import numpy as np, ml_dtypes
CORES = [6,15,38,47]
N = 4
BF = ml_dtypes.bfloat16
def f(rng, *shape):
    return (rng.standard_normal(shape, dtype=np.float32) * np.exp2(rng.integers(-2, 3, shape[:-1] + (1,)))).astype(BF)
def wide(rng, *shape):
    v = f(rng, *shape).astype(np.float32); k = shape[:-2] + (1, shape[-1])
    return (v * np.exp2(rng.integers(-6, 7, k)) * (rng.random(k) > 0.0625)).astype(BF)
def gentries(a):
    return np.ascontiguousarray(a.reshape(8, 16, -1).transpose(0, 2, 1)).reshape(8, -1)
def gtable(e):
    e = np.asarray(e); return np.ascontiguousarray(e.reshape(8, -1, 16).transpose(0, 2, 1)).reshape(128, -1).astype(np.int32)
M, I, Q, W = 4096, 128, 512, 65536
CAPT, CAP = 63, 192
def parts(rng, n, lo, hi):
    room = rng.permutation(np.repeat(np.arange(len(lo)), hi - lo))[:n - int(np.sum(lo))]
    return lo + np.bincount(room, minlength=len(lo))
def ticks(rng, kind=""):
    times = np.zeros((N, 8, M), np.int32); own = np.zeros((N, 8, M), np.int64)
    for s in range(N):
        for g in range(8):
            lo = rng.integers(0, (M - 2 * CAPT) // I + 1, I); hi = np.full(I, CAPT, np.int64); o = rng.permutation(I)
            if kind == "full":
                lo[:] = 0; lo[o[:M // CAPT]] = CAPT
            else:
                c, z = o[:2], o[2:2 + I // 16]
                if kind == "ends":
                    c, z = (np.array([0, I - 1]), o[:0]) if s % 2 == 0 else (o[:0], np.array([0, I - 1]))
                lo[c] = CAPT; lo[z] = 0; hi[z] = 0
            own[s, g] = rng.permutation(np.repeat(np.arange(I), parts(rng, M, lo, hi)))
            t = rng.integers(0, W, M); t = np.where(rng.random(M) < 0.5, t, t - t % (W // 64))
            if kind == "ties":
                t = np.concatenate([[0, W - 1], rng.integers(0, W, 14)])[rng.integers(0, 16, M)]
            if kind == "ends":
                if rng.random() < 0.5:
                    t[0] = 0; t[1] = W - 1
                else:
                    t = W // 4 + t // 2
            times[s, g] = s * W + np.sort(t)
    return times, own
def index(own):
    pm = np.stack([gtable(np.argsort(own[s], axis=1, kind="stable")) for s in range(N)])
    starts = np.zeros((N, 8, I + 1), np.int32)
    for s in range(N):
        for g in range(8):
            starts[s, g, 1:] = np.add.accumulate(np.bincount(own[s, g], minlength=I))
    return pm, starts
def queries(rng, times, own, full=False):
    qi = np.zeros((N, 8, Q), np.int32); qt = np.zeros((N, 8, Q), np.int32)
    for r in range(N):
        a, b = rng.choice(8, 2, replace=False)
        for g in range(8):
            lo = np.zeros(N, np.int64); hi = np.full(N, CAP, np.int64); o = (r + 1 + rng.permutation(N - 1)) % N
            if full:
                if g % 2 == 1:
                    o = np.concatenate([[r], o])
                lo[o[:Q // CAP]] = CAP
            elif g == a:
                lo[o[0]] = CAP
            elif g == b:
                hi[o[0]] = 0
            s = rng.permutation(np.repeat(np.arange(N), parts(rng, Q, lo, hi)))
            k = rng.integers(0, M, Q); u = rng.random(Q)
            i = np.where(u < 0.5, own[s, g, k], rng.integers(0, I, Q))
            t = np.where((u > 0.25) & (u < 0.75), times[s, g, k], s * W + rng.integers(0, W, Q))
            t = np.where((u > 0.4) & (u < 0.5), np.maximum(t - 1, s * W), t)
            qi[r, g] = i; qt[r, g] = t
    return qi, qt
def sparse(rng, v):
    keep = rng.random((N, 128, M), dtype=np.float32) < np.exp2(-rng.integers(1, 7, (N, 128, 1)))
    return np.where(keep, v.astype(np.float32), np.float32(0)).astype(BF)
def make(rng, kind=""):
    times, own = ticks(rng, kind); pm, starts = index(own); qi, qt = queries(rng, times, own, kind == "full")
    return {"x": sparse(rng, f(rng, N, 128, M)), "times": times, "pm": pm, "starts": starts, "qi": qi, "qt": qt}
def setup_inputs(rng):
    return make(rng)
def setup_inputs_ends(rng):
    d = make(rng, "ends"); qt = d["qt"].astype(np.int64); s = qt // W; g = np.arange(8)[None, :, None]
    first = d["times"][s, g, 0].astype(np.int64); last = d["times"][s, g, M - 1].astype(np.int64)
    c = rng.integers(0, 6, qt.shape)
    t = np.choose(c, [s * W, s * W + W - 1, np.maximum(first - 1, s * W), np.minimum(last + 1, s * W + W - 1), last, qt])
    e = rng.random(qt.shape)
    d["qi"] = np.where(e < 0.25, 0, np.where(e < 0.5, I - 1, d["qi"])).astype(np.int32); d["qt"] = t.astype(np.int32); return d
def setup_inputs_full(rng):
    return make(rng, "full")
def setup_inputs_ties(rng):
    return make(rng, "ties")
def setup_inputs_old(rng):
    d = make(rng); h = np.where(rng.random(128) < 0.5, 0, rng.integers(0, N, 128))
    keep = (np.arange(N)[:, None] == h)[:, :, None] & (rng.random((N, 128, M), dtype=np.float32) < 0.25)
    d["x"] = np.where(keep, f(rng, N, 128, M).astype(np.float32), np.float32(0)).astype(BF); return d
def setup_inputs_spread(rng):
    d = make(rng); d["x"] = sparse(rng, wide(rng, N, 128, M)); return d
def check_inputs(d):
    bad = []; t = d["times"].astype(np.int64); st = d["starts"].astype(np.int64); qi = d["qi"]; qt = d["qt"].astype(np.int64)
    e = np.stack([gentries(a) for a in d["pm"]]).astype(np.int64); s0 = (np.arange(N) * W)[:, None, None]
    size = np.abs(d["x"].astype(np.float32))
    if not np.isfinite(size).all(): bad.append("x finite")
    if not ((size == 0) | (size >= 2.0 ** -100)).all(): bad.append("x size")
    if not ((t >= s0) & (t < s0 + W)).all(): bad.append("times in the slice")
    if not (np.diff(t, axis=2) >= 0).all(): bad.append("times in order")
    n = np.diff(st, axis=2)
    if not ((st[:, :, 0] == 0).all() and (st[:, :, I] == M).all() and (n >= 0).all()): bad.append("starts")
    else:
        if not (n <= CAPT).all(): bad.append("ticks of an instrument")
        for s in range(N):
            for g in range(8):
                edge = np.zeros(M + 1, bool); edge[st[s, g]] = True
                if not ((np.diff(e[s, g]) > 0) | edge[1:M]).all() and "pm in order" not in bad: bad.append("pm in order")
    if not (np.sort(e, axis=2) == np.arange(M)).all(): bad.append("pm a permutation")
    if not ((qi >= 0) & (qi < I)).all(): bad.append("qi range")
    if not ((qt >= 0) & (qt < N * W)).all(): bad.append("qt range")
    if not all((np.sum(qt // W == s, axis=2) <= CAP).all() for s in range(N)): bad.append("queries in a slice")
    return bad
def reference(x, times, pm, starts, qi, qt):
    y = np.zeros((N, 8, 16, Q), np.float32)
    for g in range(8):
        i = qi[:, g].reshape(-1).astype(np.int64); key = i * (N * W) + qt[:, g].reshape(-1)
        v = np.zeros((16, N * Q), np.float32)
        for s in range(N):
            e = gentries(pm[s])[g]; st = starts[s, g].astype(np.int64)
            w = x[s, 16 * g:16 * g + 16].astype(np.float32)[:, e]
            p = np.searchsorted(np.repeat(np.arange(I), np.diff(st)) * (N * W) + times[s, g][e], key, "right")
            last = np.maximum.accumulate(np.where(w != 0, np.arange(M), -1), axis=1)
            last = np.concatenate([np.full((16, 1), -1, np.int64), last], axis=1)[:, p]
            v = np.where(last >= st[i], np.take_along_axis(w, np.maximum(last, 0), axis=1), v)
        y[:, g] = v.reshape(16, N, Q).transpose(1, 0, 2)
    return {"y": y.reshape(N, 128, Q).astype(BF)}

@@ -1,0 +1,348 @@
+from concourse.bass import DstId, RemoteDMATransfer
+from concourse.mybir import AluOpType as A, ActivationFunctionType as F
+
+M, Q, CAP, W = 4096, 512, 192, 65536
+BIG = float(2 ** 20)
+BF, F32, I32, U16 = "bfloat16", "float32", "int32", "uint16"
+COLS = {
+    BF: dict(bb=128, b12=128, lin=128, eye=128, z=144, z0=144, za1=144, za2=144, pcs=128, qtr=64, oh=136, rst=136, sc=136,
+             rows=512, sw=768, tp=512, tw=M, tsw=4240, bt=128, fs=128, xw=M, xs=M, mk=4240, ff=4240, lq=768, ca=768,
+             cb=768, gb=768, ob=768, land=768, ll=384, sg=384, cw=512, m1=256, c1=256, v=512, mv=512, cz=512, yo=512),
+    F32: dict(pf=16, bc=8, iob=128, ioz=144, ios=24, io5=8, qf=64, prod=136, t1=72, slf=96, em=24,
+              l2f=16, wf=384, pen=768, kw=528, ta=768, qw=768),
+    I32: dict(ip=2, pg=2, qp=64, qw1=96, tb=256, pmi=256, stb=16, b0c=8, srow=536),
+    U16: dict(slot=32, coff=32, pmu=256, l2=16, l5=48, ls=24, offa=48, offb=48, offf=48),
+}
+PS = ("pk", "pk2", "pq1", "pq2", "pb", "pp", "pi", "pfi")
+SCRATCH = {n: ("sbuf", [128, c], d) for d in COLS for n, c in COLS[d].items()}
+SCRATCH.update({n: ("psum", [128, 512], F32) for n in PS})
+SEMAPHORES = ["ev", "es", "et", "eg", "qa", "la", "ra", "loc"] + ["d%d" % k for k in range(16)]
+
+
+def rank_program(g, core, T, topo):
+    r = T.rank_of(core)
+    if r is None:
+        return
+    cores = list(T.cores)
+    N = len(cores)
+    qs = {"v": g.vector, "s": g.scalar, "t": g.tensor, "g": g, "y": g.sync}
+    esem = {"v": "ev", "s": "es", "t": "et", "g": "eg"}
+    cnt, seen, wr, rd, nd = {}, {}, {}, {}, [0]
+
+    def wait(e, tok):
+        if seen.get((e, tok[0]), 0) < tok[1]:
+            qs[e].wait_ge(T.sem[tok[0]], tok[1])
+            seen[(e, tok[0])] = tok[1]
+
+    def deps(e, R, Wr):
+        toks = {}
+        for t in [t for k in R + Wr for t in wr.get(k, [])] + [t for k in Wr for t in rd.get(k, [])]:
+            toks[t[0]] = max(toks.get(t[0], 0), t[1])
+        for s in toks:
+            wait(e, (s, toks[s]))
+
+    def note(tok, R, Wr):
+        for k in R:
+            rd.setdefault(k, []).append(tok)
+        for k in Wr:
+            wr[k] = [tok]
+            rd[k] = []
+
+    def op(e, fn, R, Wr):
+        R, Wr = R.split(), Wr.split()
+        for k in R:
+            if k in PS:
+                for t in rd.get(k, []):
+                    if t[0] != esem[e]:
+                        wait(e, t)
+        deps(e, R, Wr)
+        s = esem[e]
+        fn().then_inc(T.sem[s], 1)
+        cnt[s] = cnt.get(s, 0) + 1
+        note((s, cnt[s]), R, Wr)
+
+    def dmas(items):
+        s = "d%d" % nd[0]
+        nd[0] += 1
+        for e, o, i, R, Wr in items:
+            deps(e, R.split(), Wr.split())
+        for e, o, i, R, Wr in items:
+            qs[e].dma_start(o, i).then_inc(T.sem[s], 16)
+        cnt[s] = 16 * len(items)
+        for e, o, i, R, Wr in items:
+            note((s, cnt[s]), R.split(), Wr.split())
+
+    V, SC, PE = g.vector, g.scalar, g.tensor
+
+    def ts(o, i, a, o0, R, Wr, b=None, o1=None):
+        if b is None:
+            op("v", lambda: V.tensor_scalar(o, i, a, None, o0), R, Wr)
+        else:
+            op("v", lambda: V.tensor_scalar(o, i, a, b, o0, o1), R, Wr)
+
+    def tt(o, a, b, o0, R, Wr):
+        op("v", lambda: V.tensor_tensor(o, a, b, o0), R, Wr)
+
+    def cp(o, i, R, Wr):
+        op("v", lambda: V.tensor_copy(o, i), R, Wr)
+
+    def ms(o, c, Wr):
+        op("v", lambda: V.memset(o, c), "", Wr)
+
+    def scan(o, a, b, ini, R, Wr):
+        op("v", lambda: V.tensor_tensor_scan(o, a, b, ini, A.mult, A.add), R, Wr)
+
+    def act(o, i, R, Wr, f=F.Copy, **kw):
+        op("s", lambda: SC.activation(o, i, f, **kw), R, Wr)
+
+    def lin(o, i, sc, bi, R, Wr):
+        act(o, i, R, Wr, F.Identity, scale=sc, bias=bi)
+
+    def iota(o, pat, base, Wr):
+        op("g", lambda: g.iota(o, pat, base, 0, allow_small_or_imprecise_dtypes=True), "", Wr)
+
+    def sel(o, i, pat, cmp, cm, R, Wr):
+        op("g", lambda: g.affine_select(o, i, pat, cmp, 0.0, 0, cm), R, Wr)
+
+    def mm(calls, R, Wr):
+        op("t", lambda: [PE.matmul(*c) for c in calls][-1], R, Wr)
+
+    def spread(out, z, src, lo, hi, first, last):
+        return [(out, z[:, 15 - k:143 - k], src[:, lo + k:hi:16], first and k == 0, last and k == 15) for k in range(16)]
+
+    def far(p):
+        a, b = topo.chip(core), topo.chip(cores[p])
+        return 2 if a == b else 1 if topo.mates(a, b) or topo.same_plane(a, b) else 0
+    peers = sorted([p for p in range(N) if p != r], key=far)
+
+    def width(a, b):
+        return len(topo.engines(cores[a], cores[b]))
+
+    def common(a):
+        return [e for e in topo.engines(cores[a], cores[(a + 1) % N])
+                if all(e in topo.engines(cores[a], cores[b]) for b in range(N) if b != a)]
+
+    def send(p, dst, src, sem, R):
+        deps("g", R.split(), [])
+        rid, pid, se = topo.addr(cores[p])
+        g.remote_dma(dst, src, T.sem[sem], T.sem.loc, pid, rid, topo.mask(core, cores[p]))
+        cnt["loc"] = cnt.get("loc", 0) + width(r, p)
+    arrive = sum(width(p, r) for p in peers)
+    pf, wf = T.pf, T.wf
+    G16, P16, P8, A128, E4, W12, W0, WA2, SA, BA = [pf[:, k:k + 1] for k in range(10)]
+    TW = "tw0 tw1 tw2 tw3"
+
+    ms(T.tw[:, 0:1024], 0.0, "tw0")
+    dmas([("y", T.qp[:, 0:16], T.qt[0::2, :], "", "qp"), ("y", T.qp[:, 16:32], T.qt[1::2, :], "", "qp"),
+          ("s", T.qp[:, 32:48], T.qi[0::2, :], "", "qp"), ("s", T.qp[:, 48:64], T.qi[1::2, :], "", "qp")])
+    dmas([("s", T.tb[:], T.times[:], "", "tb")])
+    dmas([("y", T.pmi[:], T.pm[:], "", "pmi")])
+    dmas([("s", T.stb[:, 0:8], T.starts[:, 0:128], "", "stb"), ("s", T.stb[:, 8:16], T.starts[:, 1:129], "", "stb")])
+    op("g", lambda: g.iota(T.ip[:, 0:1], [[1, 1]], 0, 1), "", "ip")
+    iota(T.iob[:], [[16, 8], [0, 16]], 0, "iob")
+    iota(T.ioz[:], [[1, 144]], -15, "ioz")
+    op("g", lambda: g.iota(T.srow[:, 0:136], [[0, 136]], 0, 0), "", "srow")
+    dmas([("y", T.srow[0::16, 0:129], T.starts[:], "", "srow")])
+    iota(T.oh[:, 0:132:33], [[12, 4]], 0, "ohl")
+    act(T.tw[:, 1024:2048], T.tw[:, 0:1024], "tw0", "tw1")
+    act(T.tw[:, 2048:3072], T.tw[:, 0:1024], "tw0", "tw2")
+    act(T.tw[:, 3072:3584], T.tw[:, 0:512], "tw0", "tw2")
+    ms(T.tw[:, 3584:M], 0.0, "tw3")
+    ts(T.pg[:, 0:1], T.ip[:, 0:1], 112, A.bitwise_and, "ip", "pg0")
+    ts(T.pg[:, 1:2], T.ip[:, 0:1], 15, A.bitwise_and, "ip", "pg1")
+    ms(T.rst[:], 1.0, "rst")
+    cp(pf[:, 0:2], T.pg[:], "pg0 pg1", "pf")
+    ms(T.rows[:], 0.0, "rows")
+    ms(T.rst[:, 0:132:33], 0.0, "rst")
+    ts(T.bb[:], T.iob[:], G16, A.is_equal, "iob pf", "bb")
+    sel(T.lin[:], T.bb[:], [[1, 128]], A.is_ge, -1, "bb", "lin")
+    iota(T.sw[:], [[0, 768]], 0, "sw")
+    iota(T.ios[:], [[136, 3], [1, 8]], 0, "ios")
+    iota(T.io5[:, 0:5], [[16, 5]], 0, "io5")
+    iota(T.tsw[:, M:4240], [[0, 144]], W, "tsp")
+    iota(T.cw[:, 0:128], [[0, 128]], 0, "cw0")
+    iota(T.ff[:, M + 1:4240], [[0, 143]], 0, "ffp")
+    iota(T.ff[:, 0:1], [[0, 1]], 0, "ff")
+    ts(A128, P16, 3.0, A.is_le, "pf", "a128", 128.0, A.mult)
+    ts(E4, P16, 4.0, A.is_equal, "pf", "e4", -8192.0, A.mult)
+    ts(T.z[:], T.ioz[:], G16, A.is_equal, "ioz pf", "z")
+
+    ts(T.qw1[:, 0:32], T.qp[:, 0:32], W - 1, A.bitwise_and, "qp", "tl")
+    ts(T.qw1[:, 32:64], T.qp[:, 32:64], 3, A.arith_shift_right, "qp", "i8")
+    ts(T.qf[:, 0:32], T.qp[:, 32:64], 16.0, A.mult, "qp", "qfa")
+    cp(T.pcs[:, 0:32], T.qw1[:, 0:32], "tl", "hi")
+    ts(T.qf[:, 32:64], T.qw1[:, 32:64], -127.0, A.mult, "i8", "qfb")
+    tt(T.pcs[:, 32:64], T.qw1[:, 0:32], T.pcs[:, 0:32], A.subtract, "tl hi", "lo")
+    tt(T.pcs[:, 64:96], T.qf[:, 0:32], T.qf[:, 32:64], A.add, "qfa qfb", "inst")
+    dmas([("y", T.rows[16 * h + row::32, :], T.pcs[:, c0 + 16 * h:c0 + 16 * h + 16], key, "rows")
+          for row, c0, key in ((1, 0, "hi"), (2, 32, "lo"), (0, 64, "inst")) for h in range(2)])
+    ts(T.tp[:, 0:256], T.tb[:], float(r * W), A.subtract, "tb", "tph")
+    ts(T.pk[:, 0:256], T.tb[:], float(r * W), A.subtract, "tb", "pk")
+    ts(T.qw1[:, 64:96], T.qp[:, 0:32], 16, A.arith_shift_right, "qp", "si")
+    tt(T.tp[:, 256:512], T.pk[:, 0:256], T.tp[:, 0:256], A.subtract, "pk tph", "tpl")
+    dmas([("y", T.tw[0::16, :], T.tp[:, 0:256], "tph", TW), ("y", T.tw[1::16, :], T.tp[:, 256:512], "tpl", TW)])
+    dmas([("y", T.xw[:], T.x[:], "", "xw")])
+    cp(T.pcs[:, 96:128], T.qw1[:, 64:96], "si", "sf")
+    op("v", lambda: V.transpose(T.qtr[:], T.pcs[:, 64:128]), "inst sf", "qtr")
+    ts(T.b0c[:], T.stb[:, 0:8], 4, A.arith_shift_right, "stb", "b0c")
+    for s in range(4):
+        ts(T.oh[:, 33 * s + 1:33 * s + 33], T.qtr[:, 32:64], float(s), A.is_equal, "qtr", "ohb%d" % s)
+    ohk = "ohl ohb0 ohb1 ohb2 ohb3"
+    scan(T.sc[:, 0:132], T.rst[:, 0:132], T.oh[:, 0:132], 0.0, "rst " + ohk, "sc")
+    mm([(T.pi[:, 0:131], T.lin[:], T.oh[:, 1:132], True, False), (T.pi[:, 0:131], T.bb[:], T.sc[:, 0:131], False, True)],
+       "lin bb sc " + ohk, "pi")
+    cp(T.pmu[:], T.pmi[:], "pmi", "pmu")
+    tt(T.prod[:, 0:131], T.pi[:, 0:131], T.oh[:, 1:132], A.mult, "pi " + ohk, "prod")
+    tt(T.t1[:, 0:65], T.prod[:, 0:65], T.prod[:, 66:131], A.add, "prod", "t1")
+    tt(T.slf[:, 0:32], T.t1[:, 0:32], T.t1[:, 33:65], A.add, "t1", "slf")
+    ts(T.slot[:], T.slf[:, 0:32], 1.0, A.subtract, "slf", "slot")
+    cp(T.sw[:].indirect(T.slot[:]), T.rows[:], "slot rows", "sw")
+    for p in peers:
+        send(p, T.lq[:, CAP * r:CAP * (r + 1)], T.sw[:, CAP * p:CAP * (p + 1)], "qa", "sw")
+    sel(T.lq[:, CAP * r:CAP * (r + 1)], T.sw[:, CAP * r:CAP * (r + 1)], [[0, CAP]], A.is_ge, 0, "sw", "lqo")
+    sel(T.eye[:], T.bb[:], [[1, 128]], A.is_equal, -1, "bb", "eye")
+    lin(P8, P16, 8.0, 0.0, "pf", "p8")
+    act(W12, P16, "pf", "w12", F.Sign)
+    lin(SA, A128, BIG / 128, 0.0, "a128", "sa")
+    lin(BA, P16, 16.0, 16.0, "pf", "ba")
+    lin(WA2, A128, 0.125, E4, "a128 e4", "wa2")
+    lin(W0, W12, -1.0, 1.0, "w12", "w0")
+    lin(T.b12[:], T.bb[:], W12, 0.0, "bb w12", "b12")
+    lin(T.z0[:], T.z[:], W0, 0.0, "z w0", "z0")
+    lin(T.za1[:], T.z[:], A128, 0.0, "z a128", "za1")
+    lin(T.za2[:], T.z[:], WA2, 0.0, "z wa2", "za2")
+    lin(T.bc[:, 0:5], T.io5[:, 0:5], 1.0, P16, "io5 pf", "bc")
+    lin(T.em[:, 8:16], T.ios[:, 0:8], 1.0, P8, "ios p8", "dj")
+    ts(T.srow[:, 272:408], T.srow[:, 0:136], 8176, A.bitwise_and, "srow", "sb")
+    ts(T.srow[:, 136:272], T.srow[:, 0:136], 15, A.bitwise_and, "srow", "sr")
+    ts(T.ls[:], T.ios[:], P8, A.add, "ios p8", "ls")
+    tt(T.srow[:, 408:536], T.srow[:, 1:129], T.srow[:, 272:400], A.subtract, "srow sb", "sd")
+    cp(T.sg[:], T.srow[:, 136:536].indirect(T.ls[:]), "sr sb sd ls", "sg")
+
+    def tchunk(c, f):
+        f(T.tsw[:, 1024 * c:1024 * (c + 1)], T.tw[:].indirect(T.pmu[:, 64 * c:64 * (c + 1)]), TW + " pmu", "ts%d" % c)
+
+    def kchunk(c):
+        hi = 1024 * (c + 1) + (128 if c == 3 else 0)
+        mm(spread(T.pk[:, 64 * c:hi // 16], T.z, T.tsw, 1024 * c, hi, True, True), "z tsp ts%d" % c, "pk")
+
+    def k2(a, b, R):
+        mm([(T.pk2[:, a:b], T.z[:, 15 - k:143 - k], T.tsw[:, 16 * (a + k + 1):16 * (b + k) + 1:16], k == 0, k == 3)
+            for k in range(4)], "z " + R, "pk2")
+    tchunk(0, act)
+    kchunk(0)
+    mm([(T.pp[:, 0:384], T.bb[:], T.sg[:], True, True)], "bb sg", "pp")
+    tchunk(3, cp)
+    tt(T.em[:, 0:8], T.stb[:, 8:16], T.stb[:, 0:8], A.is_le, "stb", "em")
+    ts(T.em[:, 8:16], T.em[:, 8:16], float(M + 1), A.add, "dj", "dj")
+    for c in range(6):
+        ts(T.l5[:, 8 * c:8 * c + 8], T.b0c[:], float(c if c < 5 else 264), A.add, "b0c", "l5%d" % c)
+        if c == 0:
+            tt(T.em[:, 16:24], T.em[:, 0:8], T.em[:, 8:16], A.mult, "em dj", "ed")
+        if c == 1:
+            tt(T.l2f[:, 0:8], T.em[:, 16:24], T.stb[:, 0:8], A.max, "ed stb", "l2a")
+            tt(T.l2f[:, 8:16], T.em[:, 16:24], T.stb[:, 8:16], A.max, "ed stb", "l2b")
+        if c == 2:
+            cp(T.l2[:], T.l2f[:], "l2a l2b", "l2")
+    D = T.pp[:, 256:384]
+    ts(wf[:, 0:128], D, T.bc[:, 0:1], A.is_le, "pp bc", "pa", BIG, A.mult)
+    ts(wf[:, 128:256], T.pp[:, 0:128], P16, A.is_gt, "pp pf", "pc", BIG, A.mult)
+    for c in range(1, 5):
+        ts(T.pen[:, 128 * c:128 * (c + 1)], D, T.bc[:, c:c + 1], A.is_le, "pp bc", "pen%d" % c, BIG, A.mult)
+    ts(wf[:, 256:384], D, BA, A.is_le, "pp sa ba", "pd", SA, A.mult)
+    cp(T.bt[:], T.pp[:, 128:256], "pp", "bt")
+    tt(T.pen[:, 0:128], wf[:, 0:128], wf[:, 128:256], A.subtract, "pa pc", "pen0")
+    tchunk(1, act)
+    kchunk(1)
+    k2(0, 124, "ts0 ts1")
+    kchunk(3)
+    k2(191, 258, "ts3 tsp")
+    tchunk(2, act)
+    act(T.fs[:], T.tsw[:].indirect(T.l2[:, 0:8]), "ts0 ts1 ts2 ts3 tsp l2", "fs")
+    kchunk(2)
+    k2(124, 191, "ts1 ts2 ts3")
+    mm([(T.pfi[:, 0:128], T.z[:, 11:139], T.fs[:], True, True)], "z fs", "pfi")
+    wr["lqr"] = [("qa", arrive)]
+    cnt["qa"] = arrive
+    mm([(T.pq1[:, 0:384], T.b12[:], T.lq[:, 0:384], True, True)], "b12 lqo lqr", "pq1")
+    mm([(T.pq2[:, 0:384], T.b12[:], T.lq[:, 384:768], True, True)], "b12 lqo lqr", "pq2")
+    mm(spread(T.pi[:, 0:48], T.z0, T.lq, 0, 768, True, True), "z0 lqo lqr", "pi")
+    mm(spread(T.pb[:, 0:48], T.z0, T.lq, 0, 768, True, False), "z0 lqo lqr", "pb")
+
+    def xchunk(c):
+        act(T.xs[:, 1024 * c:1024 * (c + 1)], T.xw[:].indirect(T.pmu[:, 64 * c:64 * (c + 1)]), "xw pmu", "xs%d" % c)
+
+    def fill(a, b):
+        keys = " ".join("xs%d" % c for c in range(a // 1024, b // 1024))
+        ts(T.mk[:, a:b], T.xs[:, a:b], 0.0, A.is_equal, keys, "mk")
+        cp(T.mk[:].indirect(T.l2[:, 0:8]), T.cw[:, 0:128], "l2 cw0", "mk")
+        scan(T.ff[:, a + 1:b + 1], T.mk[:, a:b], T.xs[:, a:b], T.ff[:, a:a + 1] if a else 0.0, "mk ff " + keys, "ff")
+    xchunk(0)
+    act(T.qw[:, 0:384], T.pq1[:, 0:384], "pq1", "qw0")
+    act(T.qw[:, 384:768], T.pq2[:, 0:384], "pq2", "qw1")
+    xchunk(1)
+    cp(T.kw[:, 0:264], T.pk[:, 0:264], "pk", "kwa")
+    cp(T.kw[:, 264:522], T.pk2[:, 0:258], "pk2", "kwb")
+    tt(T.pen[:, 640:768], T.pfi[:, 0:128], wf[:, 256:384], A.add, "pfi pd", "pen5")
+    tt(T.ta[:], T.kw[:, 0:522].indirect(T.l5[:]), T.pen[:], A.add,
+       "kwa kwb l50 l51 l52 l53 l54 l55 pen0 pen1 pen2 pen3 pen4 pen5", "ta")
+    cp(T.offa[:], T.pi[:, 0:48], "pi", "offa")
+    tt(T.ca[:], T.ta[:, 640:768].indirect(T.offa[:]), T.qw[:], A.is_le, "ta offa qw0 qw1", "ca")
+    xchunk(2)
+    xchunk(3)
+    act(T.gb[:], T.bt[:].indirect(T.offa[:]), "bt offa", "gb")
+    mm(spread(T.pb[:, 0:48], T.za1, T.ca, 0, 768, False, True), "za1 ca", "pb")
+    mm(spread(T.pp[:, 0:48], T.za2, T.ca, 0, 768, True, False), "za2 ca", "pp")
+    fill(0, 2048)
+    fill(2048, M)
+    fw = T.ff[:]
+
+    def last(s):
+        return T.cw[:, 128:256] if s == 0 else T.ll[:, 128 * s:128 * s + 128]
+    if r < N - 1:
+        cp(last(r), fw.indirect(T.l2[:, 8:16]), "ff ffp l2", "lol")
+        deps("g", ["lol"], [])
+        to = [DstId(rid=topo.addr(cores[p])[0], pnc=topo.addr(cores[p])[1]) for p in peers]
+        g.remote_dma_fused([RemoteDMATransfer(dst_ids=to, dma_engine_mask=sum(1 << e for e in common(r)), remote_sem=T.sem.la,
+                                              src=last(r), dsts=[last(r)] * len(peers))], local_sem=T.sem.loc)
+        cnt["loc"] += len(common(r))
+    cp(T.offb[:], T.pb[:, 0:48], "pb", "offb")
+    tt(T.cb[:], T.ta[:, 0:640].indirect(T.offb[:]), T.qw[:], A.is_le, "ta offb qw0 qw1", "cb")
+    mm(spread(T.pp[:, 0:48], T.z0, T.gb, 0, 768, False, False), "z0 gb", "pp")
+    mm(spread(T.pp[:, 0:48], T.z, T.cb, 0, 768, False, True), "z cb", "pp")
+    lin(T.slf[:, 32:64], T.qtr[:, 32:64], 128.0, 0.0, "qtr", "s128")
+    tt(T.slf[:, 64:96], T.slf[:, 32:64], T.qtr[:, 0:32], A.add, "qtr s128", "cof")
+    cp(T.coff[:], T.slf[:, 64:96], "cof", "coff")
+    ts(T.offf[:], T.pp[:, 0:48], 8192.0, A.add, "pp", "offf", float(M + 1), A.min)
+
+    for n, p in enumerate(peers):
+        (cp if n == 1 else act)(T.ob[:, CAP * p:CAP * (p + 1)], fw.indirect(T.offf[:, 12 * p:12 * p + 12]), "ff ffp offf", "oa%d" % p)
+        send(p, T.land[:, CAP * r:CAP * (r + 1)], T.ob[:, CAP * p:CAP * (p + 1)], "ra", "oa%d" % p)
+    cp(T.land[:, CAP * r:CAP * (r + 1)], fw.indirect(T.offf[:, 12 * r:12 * r + 12]), "ff ffp offf", "loa")
+    cnt["la"] = sum(len(common(p)) for p in peers if p < N - 1)
+    wr["llr"] = [("la", cnt["la"])]
+    LK = "llr lol"
+    ts(T.m1[:], T.ll[:, 128:384], 0.0, A.is_equal, LK, "m1")
+    tt(T.c1[:, 0:128], T.m1[:, 0:128], last(0), A.mult, LK + " m1", "c1")
+    tt(T.cw[:, 256:384], T.c1[:, 0:128], last(1), A.add, LK + " c1", "cw2")
+    tt(T.c1[:, 128:256], T.m1[:, 128:256], T.cw[:, 256:384], A.mult, "m1 cw2", "c2")
+    tt(T.cw[:, 384:512], T.c1[:, 128:256], last(2), A.add, LK + " c2", "cw3")
+    cp(T.cz[:], T.cw[:].indirect(T.coff[:]), LK + " cw0 cw2 cw3 coff", "cg")
+    cp(T.pk[:], T.cz[:], "cg", "pk")
+    wr["lar"] = [("ra", arrive)]
+    cnt["ra"] = arrive
+    pv = (T.pq1[:, 0:256], T.pq2[:, 0:256])
+    for h in range(2):
+        c = slice(256 * h, 256 * (h + 1))
+        win = T.land[:].indirect(T.slot[:, 16 * h:16 * (h + 1)])
+        act(T.v[:, c], win, "lar loa slot", "v%d" % h)
+        mm([(pv[h], T.eye[:], T.v[:, c], True, h == 1)], "eye v%d" % h, "pq%d" % (h + 1))
+        ts(T.mv[:, c], win, 0.0, A.is_equal, "lar loa slot", "mv%d" % h)
+        tt(T.cz[:, c], T.pk[:, c], T.mv[:, c], A.mult, "pk cg mv%d" % h, "cz%d" % h)
+    mm([(pv[0], T.eye[:], T.cz[:, 0:256], False, True)], "eye cz0", "pq1")
+    act(T.yo[:, 0:256], pv[0], "pq1", "yo0")
+    dmas([("s", T.y[:, 0:256], T.yo[:, 0:256], "yo0", "")])
+    tt(T.yo[:, 256:512], pv[1], T.cz[:, 256:512], A.add, "pq2 cz1", "yo1")
+    dmas([("y", T.y[:, 256:512], T.yo[:, 256:512], "yo1", "")])
+    for s in cnt:
+        wait("g", (s, cnt[s]))

@@ -2,21 +2,39 @@ from concourse.bass import DstId, RemoteDMATransfer
 from concourse.mybir import AluOpType as A, ActivationFunctionType as F
 
 M, Q, CAP, W = 4096, 512, 192, 65536
+PAD = M + 256
 BIG = float(2 ** 20)
+RND = 1.5 * 2 ** 23
 BF, F32, I32, U16 = "bfloat16", "float32", "int32", "uint16"
 COLS = {
-    BF: dict(bb=128, b12=128, lin=128, eye=128, z=144, z0=144, za1=144, za2=144, pcs=128, qtr=64, oh=136, rst=136, sc=136,
-             rows=512, sw=768, tp=512, tw=M, tsw=4240, bt=128, fs=128, xw=M, xs=M, mk=4240, ff=4240, lq=768, ca=768,
-             cb=768, gb=768, ob=768, land=768, ll=384, sg=384, cw=512, m1=256, c1=256, v=512, mv=512, cz=512, yo=512),
-    F32: dict(pf=16, bc=8, iob=128, ioz=144, ios=24, io5=8, qf=64, prod=136, t1=72, slf=96, em=24,
-              l2f=16, wf=384, pen=768, kw=528, ta=768, qw=768),
-    I32: dict(ip=2, pg=2, qp=64, qw1=96, tb=256, pmi=256, stb=16, b0c=8, srow=536),
-    U16: dict(slot=32, coff=32, pmu=256, l2=16, l5=48, ls=24, offa=48, offb=48, offf=48),
+    BF: dict(one=128, kn=128, bb=128, b12=128, lin=128, eye=128, z=144, z0=144, za1=144, za2=144, pcs=96, oh=136, rst=136,
+             sc=136, rows=512, u=1344, tp=512, tw=M, tsw=PAD, rd0=384, nb=128, pen=640, pa=256, pd=128, fs=128, xw=M, xs=M,
+             mk=PAD, ff=PAD, ca=768, cb=768, a=1344, lo=128, ll=384, il=512, zl=512, cw=512, iv=1024, zv=1024,
+             ov=1024, yo=512, zero=128, offab=48),
+    F32: dict(pf=8, c0=32, cd=128, cr=160, ct=160, qf=96, qtr=96, prod=136, t1=72, slf=96, sf=136, sx=136, dj=8, em=32, lf=64,
+              ub=128, kwa=264, kwb=264, pen5=128, ta1=128, ta2=640, qw=768),
+    I32: dict(qp=128, qn=32, qm=96, tb=256, pmi=256, srow=136),
+    U16: dict(slot=32, coff=32, pmu=256, l5=64, offa=48, offb=48, offf=48),
 }
 PS = ("pk", "pk2", "pq1", "pq2", "pb", "pp", "pi", "pfi")
 SCRATCH = {n: ("sbuf", [128, c], d) for d in COLS for n, c in COLS[d].items()}
 SCRATCH.update({n: ("psum", [128, 512], F32) for n in PS})
-SEMAPHORES = ["ev", "es", "et", "eg", "qa", "la", "ra", "loc"] + ["d%d" % k for k in range(16)]
+SEMAPHORES = ["ev", "es", "et", "eg", "qa", "la", "ra", "loc"] + ["d%d" % k for k in range(20)]
+XA = 512
+TCH = ((0, 1024, "s"), (1024, 2048, "s"), (2048, 2816, "s"), (3072, M, "v"), (2816, 3072, "v"))
+XCH = ((0, 512, "s"), (512, 1024, "s"), (1024, 2048, "s"), (2048, 3072, "s"), (3072, 3584, "v"), (3584, M, "s"))
+MCH = ((0, 1024), (1024, 2048), (2048, M))
+FCH = ((0, M),)
+ORDER = dict(
+    y="Ltb Lst0 Lst1 Lst2 Lst3 Lsrow Lpm Dtw0 Dtw1 Drow0 Drow1 Drow2 Lxa Lxb Y0",
+    s="Lqt0 Lqt1 Lqi0 Lqi1 Lqn Lqm tw0 tw1 tw2 tw3 rst sw sw2 rst0 sx b0 b16p b16 b0x T0 T1024 T2048 lf0 lf1 lf2 lf3 lf4 "
+      "ba ub pa pc pd nb pen1 pen2 pen3 pen4 X0 X512 qw0 qw1 offab X1024 X2048 X3584 qi4 lo oa1 oa3 il2 il3 cz0 v0 yo1 Y1",
+    v="st rows srow tw4 tph tpf si tpl low hi qf sf qtr pcs oh0 oh1 oh2 oh3 sc pmu rd0 prod rd1 t1 em slf ed slot pad scat "
+      "lf5 T3072 cr0 lf6 ct T2816 X3072 l5 fs pen0 kwa kwb pen5 ta2 ta1 offa ca M0 za2 M1024 offb cb M2048 cof R0 coff F0 offf "
+      "oa0 oa2 zl2 il1 zl3 cw cz1 v1 zv1 zv0 ov1 ov0 yo0",
+    t="slotm bc K0 K1024 P0 K3072 P191 K2048 P124 pfi q1 q2 pi pb pp1 pp2",
+    g="one bb0 bb ohl lin dj z zs kn c0 cd0 cd1 cd2 cd3 cd4 cr1 cr2 cr3 Q0 Q1 Q2 eye b12 z0 za1 zero ffp ff il0 zl zv L A0 A1 A2",
+)
 
 
 def rank_program(g, core, T, topo):
@@ -27,93 +45,83 @@ def rank_program(g, core, T, topo):
     N = len(cores)
     qs = {"v": g.vector, "s": g.scalar, "t": g.tensor, "g": g, "y": g.sync}
     esem = {"v": "ev", "s": "es", "t": "et", "g": "eg"}
-    cnt, seen, wr, rd, nd = {}, {}, {}, {}, [0]
+    steps, wr, rd, bank, total = {}, {}, {}, {}, {"loc": 0}
 
-    def wait(e, tok):
-        if seen.get((e, tok[0]), 0) < tok[1]:
-            qs[e].wait_ge(T.sem[tok[0]], tok[1])
-            seen[(e, tok[0])] = tok[1]
-
-    def deps(e, R, Wr):
-        toks = {}
-        for t in [t for k in R + Wr for t in wr.get(k, [])] + [t for k in Wr for t in rd.get(k, [])]:
-            toks[t[0]] = max(toks.get(t[0], 0), t[1])
-        for s in toks:
-            wait(e, (s, toks[s]))
-
-    def note(tok, R, Wr):
-        for k in R:
-            rd.setdefault(k, []).append(tok)
-        for k in Wr:
-            wr[k] = [tok]
-            rd[k] = []
-
-    def op(e, fn, R, Wr):
+    def step(name, e, fn, R, Wr, sem, more=False):
         R, Wr = R.split(), Wr.split()
+        dep = {t for k in R + Wr for t in wr.get(k, [])} | {t for k in Wr for t in rd.get(k, [])}
+        if more:
+            dep = {t for t in dep if t in total or steps[t][0] != e}
+        for k in R + Wr:
+            b = k.split(":")[0]
+            if b in PS:
+                dep |= {t for t in bank.setdefault(b, []) if steps[t][0] != e}
+        for b in {k.split(":")[0] for k in R + Wr} & set(PS):
+            bank[b].append(name)
         for k in R:
-            if k in PS:
-                for t in rd.get(k, []):
-                    if t[0] != esem[e]:
-                        wait(e, t)
-        deps(e, R, Wr)
-        s = esem[e]
-        fn().then_inc(T.sem[s], 1)
-        cnt[s] = cnt.get(s, 0) + 1
-        note((s, cnt[s]), R, Wr)
+            rd.setdefault(k, []).append(name)
+        for k in Wr:
+            wr[k], rd[k] = [name], []
+        assert name not in steps, name
+        steps[name] = (e, fn, sem, dep)
+
+    def op(e, fn, R, Wr, n=None, more=False):
+        step(n or Wr.split()[0], e, fn, R, Wr, esem[e], more)
 
     def dmas(items):
-        s = "d%d" % nd[0]
-        nd[0] += 1
-        for e, o, i, R, Wr in items:
-            deps(e, R.split(), Wr.split())
-        for e, o, i, R, Wr in items:
-            qs[e].dma_start(o, i).then_inc(T.sem[s], 16)
-        cnt[s] = 16 * len(items)
-        for e, o, i, R, Wr in items:
-            note((s, cnt[s]), R.split(), Wr.split())
+        s = "d%d" % len(total)
+        total[s] = 16 * len(items)
+        was = {k: (wr.get(k, []), rd.get(k, [])) for it in items for k in it[5].split()}
+        for n, e, o, i, R, Wr in items:
+            for k in Wr.split():
+                wr[k], rd[k] = was[k]
+            step(n, e, lambda e=e, o=o, i=i: qs[e].dma_start(o, i), R, Wr, s)
 
     V, SC, PE = g.vector, g.scalar, g.tensor
 
-    def ts(o, i, a, o0, R, Wr, b=None, o1=None):
-        if b is None:
-            op("v", lambda: V.tensor_scalar(o, i, a, None, o0), R, Wr)
-        else:
-            op("v", lambda: V.tensor_scalar(o, i, a, b, o0, o1), R, Wr)
+    def ts(o, i, a, o0, R, Wr, b=None, o1=None, n=None):
+        op("v", lambda: V.tensor_scalar(o, i, a, None, o0) if b is None else V.tensor_scalar(o, i, a, b, o0, o1), R, Wr, n)
 
-    def tt(o, a, b, o0, R, Wr):
-        op("v", lambda: V.tensor_tensor(o, a, b, o0), R, Wr)
+    def tt(o, a, b, o0, R, Wr, n=None):
+        op("v", lambda: V.tensor_tensor(o, a, b, o0), R, Wr, n)
 
-    def cp(o, i, R, Wr):
-        op("v", lambda: V.tensor_copy(o, i), R, Wr)
+    def cp(o, i, R, Wr, n=None):
+        op("v", lambda: V.tensor_copy(o, i), R, Wr, n)
 
     def ms(o, c, Wr):
         op("v", lambda: V.memset(o, c), "", Wr)
 
-    def scan(o, a, b, ini, R, Wr):
-        op("v", lambda: V.tensor_tensor_scan(o, a, b, ini, A.mult, A.add), R, Wr)
+    def turn(o, i, R, Wr):
+        op("v", lambda: V.transpose(o, i), R, Wr)
 
-    def act(o, i, R, Wr, f=F.Copy, **kw):
-        op("s", lambda: SC.activation(o, i, f, **kw), R, Wr)
+    def scan(o, a, b, ini, R, Wr, n=None):
+        op("v", lambda: V.tensor_tensor_scan(o, a, b, ini, A.mult, A.add), R, Wr, n)
 
-    def lin(o, i, sc, bi, R, Wr):
-        act(o, i, R, Wr, F.Identity, scale=sc, bias=bi)
+    def act(o, i, R, Wr, n=None):
+        op("s", lambda: SC.activation(o, i, F.Copy), R, Wr, n)
 
-    def iota(o, pat, base, Wr):
-        op("g", lambda: g.iota(o, pat, base, 0, allow_small_or_imprecise_dtypes=True), "", Wr)
+    def lin(o, i, sc, bi, R, Wr, f=F.Identity, n=None):
+        op("s", lambda: SC.activation(o, i, f, scale=sc, bias=bi), R, Wr, n)
 
-    def sel(o, i, pat, cmp, cm, R, Wr):
-        op("g", lambda: g.affine_select(o, i, pat, cmp, 0.0, 0, cm), R, Wr)
+    def iota(o, pat, base, Wr, cm=0):
+        op("g", lambda: g.iota(o, pat, base, cm, allow_small_or_imprecise_dtypes=True), "", Wr)
 
-    def mm(calls, R, Wr):
-        op("t", lambda: [PE.matmul(*c) for c in calls][-1], R, Wr)
+    def sel(o, i, pat, cmp, base, cm, R, Wr, fill=0.0, n=None):
+        op("g", lambda: g.affine_select(o, i, pat, cmp, fill, base, cm), R, Wr, n)
+
+    def mm(n, calls, R, Wr):
+        op("t", lambda: [PE.matmul(*c) for c in calls][-1], R, Wr, n, not calls[0][3])
 
     def spread(out, z, src, lo, hi, first, last):
         return [(out, z[:, 15 - k:143 - k], src[:, lo + k:hi:16], first and k == 0, last and k == 15) for k in range(16)]
+    move = {"s": act, "v": cp}
 
-    def far(p):
-        a, b = topo.chip(core), topo.chip(cores[p])
-        return 2 if a == b else 1 if topo.mates(a, b) or topo.same_plane(a, b) else 0
-    peers = sorted([p for p in range(N) if p != r], key=far)
+    def peers_of(a):
+        def far(p):
+            x, y = topo.chip(cores[a]), topo.chip(cores[p])
+            return 2 if x == y else 1 if topo.mates(x, y) or topo.same_plane(x, y) else 0
+        return sorted([p for p in range(N) if p != a], key=far)
+    peers = peers_of(r)
 
     def width(a, b):
         return len(topo.engines(cores[a], cores[b]))
@@ -122,227 +130,234 @@ def rank_program(g, core, T, topo):
         return [e for e in topo.engines(cores[a], cores[(a + 1) % N])
                 if all(e in topo.engines(cores[a], cores[b]) for b in range(N) if b != a)]
 
-    def send(p, dst, src, sem, R):
-        deps("g", R.split(), [])
+    def send(n, p, dst, src, sem, R):
         rid, pid, se = topo.addr(cores[p])
-        g.remote_dma(dst, src, T.sem[sem], T.sem.loc, pid, rid, topo.mask(core, cores[p]))
-        cnt["loc"] = cnt.get("loc", 0) + width(r, p)
-    arrive = sum(width(p, r) for p in peers)
-    pf, wf = T.pf, T.wf
-    G16, P16, P8, A128, E4, W12, W0, WA2, SA, BA = [pf[:, k:k + 1] for k in range(10)]
-    TW = "tw0 tw1 tw2 tw3"
+        step(n, "g", lambda: g.remote_dma(dst, src, T.sem[sem], T.sem.loc, pid, rid, topo.mask(core, cores[p])), R, "", None)
+        total["loc"] += width(r, p)
 
-    ms(T.tw[:, 0:1024], 0.0, "tw0")
-    dmas([("y", T.qp[:, 0:16], T.qt[0::2, :], "", "qp"), ("y", T.qp[:, 16:32], T.qt[1::2, :], "", "qp"),
-          ("s", T.qp[:, 32:48], T.qi[0::2, :], "", "qp"), ("s", T.qp[:, 48:64], T.qi[1::2, :], "", "qp")])
-    dmas([("s", T.tb[:], T.times[:], "", "tb")])
-    dmas([("y", T.pmi[:], T.pm[:], "", "pmi")])
-    dmas([("s", T.stb[:, 0:8], T.starts[:, 0:128], "", "stb"), ("s", T.stb[:, 8:16], T.starts[:, 1:129], "", "stb")])
-    op("g", lambda: g.iota(T.ip[:, 0:1], [[1, 1]], 0, 1), "", "ip")
-    iota(T.iob[:], [[16, 8], [0, 16]], 0, "iob")
-    iota(T.ioz[:], [[1, 144]], -15, "ioz")
-    op("g", lambda: g.iota(T.srow[:, 0:136], [[0, 136]], 0, 0), "", "srow")
-    dmas([("y", T.srow[0::16, 0:129], T.starts[:], "", "srow")])
-    iota(T.oh[:, 0:132:33], [[12, 4]], 0, "ohl")
-    act(T.tw[:, 1024:2048], T.tw[:, 0:1024], "tw0", "tw1")
-    act(T.tw[:, 2048:3072], T.tw[:, 0:1024], "tw0", "tw2")
-    act(T.tw[:, 3072:3584], T.tw[:, 0:512], "tw0", "tw2")
-    ms(T.tw[:, 3584:M], 0.0, "tw3")
-    ts(T.pg[:, 0:1], T.ip[:, 0:1], 112, A.bitwise_and, "ip", "pg0")
-    ts(T.pg[:, 1:2], T.ip[:, 0:1], 15, A.bitwise_and, "ip", "pg1")
-    ms(T.rst[:], 1.0, "rst")
-    cp(pf[:, 0:2], T.pg[:], "pg0 pg1", "pf")
+    def blk(t, n):
+        return t[:, CAP * n:CAP * (n + 1)]
+
+    def keys(n, a, b):
+        return " ".join("%s.%d" % (n, c) for c in range(a // 256, (b + 255) // 256))
+    total["qa"] = total["ra"] = sum(width(p, r) for p in peers)
+    total["la"] = sum(len(common(p)) for p in peers if p < N - 1)
+    wr.update(lqr=["qa"], llr=["la"], lar=["ra"])
+
+    ms(T.qp[:, 64:96], 0, "st")
+    ms(T.srow[:], 0, "srow")
+    dmas([("Ltb", "y", T.tb[:], T.times[:], "", "tb")])
+    dmas([("Lqt%d" % h, "s", T.qp[:, 16 * h:16 * h + 16], T.qt[h::2, :], "", "qt") for h in range(2)])
+    dmas([("Lsrow", "y", T.srow[0::16, 0:129], T.starts[:], "", "srow")])
+    dmas([("Lqi%d" % h, "s", T.qp[:, 32 + 16 * h:48 + 16 * h], T.qi[h::2, :], "", "qi") for h in range(2)]
+         + [("Lst%d" % (2 * e + h), "y", T.qp[e::4, 64 + 16 * h:80 + 16 * h], T.starts[h::2, e:128 + e], "", "st")
+            for e in range(2) for h in range(2)])
+    dmas([("Lqn", "s", T.qn[:], T.qt[:], "", "qn"), ("Lqm", "s", T.qm[:, 0:32], T.qi[:], "", "qn")])
+    dmas([("Lpm", "y", T.pmi[:], T.pm[:], "", "pmi")])
+    dmas([("Lxa", "y", T.xw[:, 0:XA], T.x[:, 0:XA], "", "xwa")])
+    dmas([("Lxb", "y", T.xw[:, XA:M], T.x[:, XA:M], "", "xwb")])
     ms(T.rows[:], 0.0, "rows")
-    ms(T.rst[:, 0:132:33], 0.0, "rst")
-    ts(T.bb[:], T.iob[:], G16, A.is_equal, "iob pf", "bb")
-    sel(T.lin[:], T.bb[:], [[1, 128]], A.is_ge, -1, "bb", "lin")
-    iota(T.sw[:], [[0, 768]], 0, "sw")
-    iota(T.ios[:], [[136, 3], [1, 8]], 0, "ios")
-    iota(T.io5[:, 0:5], [[16, 5]], 0, "io5")
-    iota(T.tsw[:, M:4240], [[0, 144]], W, "tsp")
-    iota(T.cw[:, 0:128], [[0, 128]], 0, "cw0")
-    iota(T.ff[:, M + 1:4240], [[0, 143]], 0, "ffp")
+    for c in range(4):
+        n = 512 if c < 3 else 256
+        act(T.tw[:, 512 * c:512 * c + n], T.rows[:, 0:n], "rows", "tw%d" % c)
+    ms(T.tw[:, 1792:M], 0.0, "tw4")
+    TW = "tw0 tw1 tw2 tw3 tw4"
+    lin(T.rst[:], T.rows[:, 0:136], 0.0, 1.0, "rows", "rst")
+    act(T.u[:, 576:960], T.rows[:, 0:384], "rows", "sw")
+    act(T.u[:, 960:1344], T.rows[:, 0:384], "rows", "sw2")
+    ms(T.tsw[:, M:PAD], float(W), "pad")
+    iota(T.one[:], [[0, 128]], 1, "one")
+    sel(T.bb[:], T.one[:], [[-16, 8], [0, 16]], A.is_ge, 0, 1, "one", "bb", n="bb0")
+    sel(T.bb[:], T.bb[:], [[16, 8], [0, 16]], A.is_ge, 15, -1, "bb", "bb")
+    sel(T.lin[:], T.bb[:], [[1, 128]], A.is_gt, 0, -1, "bb", "lin")
+    iota(T.oh[:, 0:132:33], [[12, 4]], 0, "ohl")
+    lin(T.rst[:, 0:132:33], T.oh[:, 0:132:33], 0.0, 0.0, "ohl", "rst", n="rst0")
+    iota(T.z[:], [[0, 144]], 0, "z")
+    sel(T.z[:, 15:143:16], T.bb[:, 0::16], [[0, 8]], A.is_ge, 0, 0, "bb", "z", n="zs")
+    iota(T.kn[0:1, :], [[0, 8], [-1, 16]], 0, "kn")
+    iota(T.dj[:], [[16, 8]], M + 1, "dj", 1)
+    sel(T.b12[:], T.bb[:], [[-16, 8], [0, 16]], A.not_equal, 0, 1, "bb", "b12")
+    sel(T.z0[:], T.z[:], [[1, 144]], A.is_equal, -15, -1, "z", "z0")
+    sel(T.eye[:], T.bb[:], [[1, 128]], A.is_equal, 0, -1, "bb", "eye")
+    sel(T.za1[:], T.z[:], [[1, 144]], A.is_ge, -12, -1, "z", "za1")
+    iota(T.zero[:], [[0, 128]], 0, "zero")
+    iota(T.ff[:, M + 1:PAD], [[0, PAD - M - 1]], 0, "ffp")
     iota(T.ff[:, 0:1], [[0, 1]], 0, "ff")
-    ts(A128, P16, 3.0, A.is_le, "pf", "a128", 128.0, A.mult)
-    ts(E4, P16, 4.0, A.is_equal, "pf", "e4", -8192.0, A.mult)
-    ts(T.z[:], T.ioz[:], G16, A.is_equal, "ioz pf", "z")
+    iota(T.il[:, 0::4], [[0, 128]], 0, "il0")
+    iota(T.zl[:], [[0, 512]], 0, "zl zl2 zl3")
+    iota(T.zv[:, 0::2], [[0, 512]], 0, "zv")
+    K, KN = [[0, 2], [1, 16]], [[0, 2], [-1, 16]]
+    iota(T.c0[:], [[0, 32]], 0, "c0")
+    sel(T.cd[:, 0:32], T.c0[:], KN, A.is_ge, 5, 0, "c0", "cd0", 2.0)
+    sel(T.cd[:, 32:64], T.c0[:], KN, A.is_ge, 5, 0, "c0", "cd1", 0.5)
+    sel(T.cd[:, 64:96], T.c0[:], K, A.is_ge, -6, 0, "c0", "cd2", 16.0)
+    sel(T.cd[:, 96:128], T.c0[:], K, A.not_equal, -5, 0, "c0", "cd3", 2.0 ** 23)
+    sel(T.cd[:, 64:96], T.cd[:, 64:96], K, A.not_equal, -4, 0, "cd2", "cd2", -8192.0, "cd4")
+    sel(T.cr[:, 64:96], T.c0[:], KN, A.is_ge, 4, 0, "c0", "cr1", 2.0 ** 35 + 2.0 ** 17)
+    sel(T.cr[:, 96:128], T.c0[:], K, A.is_ge, -4, 0, "c0", "cr2", -BIG)
+    iota(T.cr[:, 128:160], [[0, 2], [-15, 16]], -17, "cr3")
+    scan(T.cr[:, 0:64], T.cd[:, 0:64], T.cd[:, 64:128], 0.0, "cd0 cd1 cd2 cd3", "cr0")
+    turn(T.ct[:], T.cr[:], "cr0 cr1 cr2 cr3", "ct")
+    WA2, SU, BU, SA, N17 = [T.ct[:, 32 * k:32 * k + 1] for k in range(5)]
+    BA = T.pf[:, 0:1]
+    lin(BA, N17, SA, 0.0, "ct", "ba")
+    ts(T.za2[:], T.z[:], WA2, A.mult, "z ct", "za2")
 
-    ts(T.qw1[:, 0:32], T.qp[:, 0:32], W - 1, A.bitwise_and, "qp", "tl")
-    ts(T.qw1[:, 32:64], T.qp[:, 32:64], 3, A.arith_shift_right, "qp", "i8")
-    ts(T.qf[:, 0:32], T.qp[:, 32:64], 16.0, A.mult, "qp", "qfa")
-    cp(T.pcs[:, 0:32], T.qw1[:, 0:32], "tl", "hi")
-    ts(T.qf[:, 32:64], T.qw1[:, 32:64], -127.0, A.mult, "i8", "qfb")
-    tt(T.pcs[:, 32:64], T.qw1[:, 0:32], T.pcs[:, 0:32], A.subtract, "tl hi", "lo")
-    tt(T.pcs[:, 64:96], T.qf[:, 0:32], T.qf[:, 32:64], A.add, "qfa qfb", "inst")
-    dmas([("y", T.rows[16 * h + row::32, :], T.pcs[:, c0 + 16 * h:c0 + 16 * h + 16], key, "rows")
-          for row, c0, key in ((1, 0, "hi"), (2, 32, "lo"), (0, 64, "inst")) for h in range(2)])
-    ts(T.tp[:, 0:256], T.tb[:], float(r * W), A.subtract, "tb", "tph")
-    ts(T.pk[:, 0:256], T.tb[:], float(r * W), A.subtract, "tb", "pk")
-    ts(T.qw1[:, 64:96], T.qp[:, 0:32], 16, A.arith_shift_right, "qp", "si")
-    tt(T.tp[:, 256:512], T.pk[:, 0:256], T.tp[:, 0:256], A.subtract, "pk tph", "tpl")
-    dmas([("y", T.tw[0::16, :], T.tp[:, 0:256], "tph", TW), ("y", T.tw[1::16, :], T.tp[:, 256:512], "tpl", TW)])
-    dmas([("y", T.xw[:], T.x[:], "", "xw")])
-    cp(T.pcs[:, 96:128], T.qw1[:, 64:96], "si", "sf")
-    op("v", lambda: V.transpose(T.qtr[:], T.pcs[:, 64:128]), "inst sf", "qtr")
-    ts(T.b0c[:], T.stb[:, 0:8], 4, A.arith_shift_right, "stb", "b0c")
-    for s in range(4):
-        ts(T.oh[:, 33 * s + 1:33 * s + 33], T.qtr[:, 32:64], float(s), A.is_equal, "qtr", "ohb%d" % s)
-    ohk = "ohl ohb0 ohb1 ohb2 ohb3"
+    ts(T.qp[:, 96:128], T.qp[:, 0:32], 16, A.arith_shift_right, "qt", "si")
+    ts(T.qm[:, 32:64], T.qn[:], 0xFF00, A.bitwise_and, "qn", "hi")
+    ts(T.qm[:, 64:96], T.qn[:], 0xFF, A.bitwise_and, "qn", "low")
+    cp(T.pcs[:], T.qm[:], "qn hi low", "pcs")
+    dmas([("Drow%d" % k, "y", T.rows[k::16, :], T.pcs[:, 32 * k:32 * k + 32], "pcs", "rows") for k in range(3)])
+    cp(T.qf[:], T.qp[:, 32:128], "qi st si", "qf")
+    turn(T.qtr[:], T.qf[:], "qf", "qtr")
+    QI, ST, EN, SI = T.qtr[:, 0:32], T.qtr[:, 32:64:4], T.qtr[:, 33:64:4], T.qtr[:, 64:96]
+    for b, s in enumerate([r] + peers):
+        ts(T.oh[:, 33 * b + 1:33 * b + 33], SI, float(s), A.is_equal, "qtr", "oh%d" % b)
+    ohk = "ohl oh0 oh1 oh2 oh3"
     scan(T.sc[:, 0:132], T.rst[:, 0:132], T.oh[:, 0:132], 0.0, "rst " + ohk, "sc")
-    mm([(T.pi[:, 0:131], T.lin[:], T.oh[:, 1:132], True, False), (T.pi[:, 0:131], T.bb[:], T.sc[:, 0:131], False, True)],
+    mm("slotm", [(T.pi[:, 0:131], T.lin[:], T.oh[:, 1:132], True, False), (T.pi[:, 0:131], T.bb[:], T.sc[:, 0:131], False, True)],
        "lin bb sc " + ohk, "pi")
-    cp(T.pmu[:], T.pmi[:], "pmi", "pmu")
     tt(T.prod[:, 0:131], T.pi[:, 0:131], T.oh[:, 1:132], A.mult, "pi " + ohk, "prod")
     tt(T.t1[:, 0:65], T.prod[:, 0:65], T.prod[:, 66:131], A.add, "prod", "t1")
     tt(T.slf[:, 0:32], T.t1[:, 0:32], T.t1[:, 33:65], A.add, "t1", "slf")
-    ts(T.slot[:], T.slf[:, 0:32], 1.0, A.subtract, "slf", "slot")
-    cp(T.sw[:].indirect(T.slot[:]), T.rows[:], "slot rows", "sw")
-    for p in peers:
-        send(p, T.lq[:, CAP * r:CAP * (r + 1)], T.sw[:, CAP * p:CAP * (p + 1)], "qa", "sw")
-    sel(T.lq[:, CAP * r:CAP * (r + 1)], T.sw[:, CAP * r:CAP * (r + 1)], [[0, CAP]], A.is_ge, 0, "sw", "lqo")
-    sel(T.eye[:], T.bb[:], [[1, 128]], A.is_equal, -1, "bb", "eye")
-    lin(P8, P16, 8.0, 0.0, "pf", "p8")
-    act(W12, P16, "pf", "w12", F.Sign)
-    lin(SA, A128, BIG / 128, 0.0, "a128", "sa")
-    lin(BA, P16, 16.0, 16.0, "pf", "ba")
-    lin(WA2, A128, 0.125, E4, "a128 e4", "wa2")
-    lin(W0, W12, -1.0, 1.0, "w12", "w0")
-    lin(T.b12[:], T.bb[:], W12, 0.0, "bb w12", "b12")
-    lin(T.z0[:], T.z[:], W0, 0.0, "z w0", "z0")
-    lin(T.za1[:], T.z[:], A128, 0.0, "z a128", "za1")
-    lin(T.za2[:], T.z[:], WA2, 0.0, "z wa2", "za2")
-    lin(T.bc[:, 0:5], T.io5[:, 0:5], 1.0, P16, "io5 pf", "bc")
-    lin(T.em[:, 8:16], T.ios[:, 0:8], 1.0, P8, "ios p8", "dj")
-    ts(T.srow[:, 272:408], T.srow[:, 0:136], 8176, A.bitwise_and, "srow", "sb")
-    ts(T.srow[:, 136:272], T.srow[:, 0:136], 15, A.bitwise_and, "srow", "sr")
-    ts(T.ls[:], T.ios[:], P8, A.add, "ios p8", "ls")
-    tt(T.srow[:, 408:536], T.srow[:, 1:129], T.srow[:, 272:400], A.subtract, "srow sb", "sd")
-    cp(T.sg[:], T.srow[:, 136:536].indirect(T.ls[:]), "sr sb sd ls", "sg")
+    cp(T.slot[:], T.slf[:, 0:32], "slf", "slot")
+    cp(T.u[:, 576:1344].indirect(T.slot[:]), T.rows[:], "slot rows", "sw sw2", "scat")
+    for n, p in enumerate(peers):
+        send("Q%d" % n, p, blk(T.u, peers_of(p).index(r)), blk(T.u, 4 + n), "qa", "sw")
 
-    def tchunk(c, f):
-        f(T.tsw[:, 1024 * c:1024 * (c + 1)], T.tw[:].indirect(T.pmu[:, 64 * c:64 * (c + 1)]), TW + " pmu", "ts%d" % c)
-
-    def kchunk(c):
-        hi = 1024 * (c + 1) + (128 if c == 3 else 0)
-        mm(spread(T.pk[:, 64 * c:hi // 16], T.z, T.tsw, 1024 * c, hi, True, True), "z tsp ts%d" % c, "pk")
-
-    def k2(a, b, R):
-        mm([(T.pk2[:, a:b], T.z[:, 15 - k:143 - k], T.tsw[:, 16 * (a + k + 1):16 * (b + k) + 1:16], k == 0, k == 3)
-            for k in range(4)], "z " + R, "pk2")
-    tchunk(0, act)
-    kchunk(0)
-    mm([(T.pp[:, 0:384], T.bb[:], T.sg[:], True, True)], "bb sg", "pp")
-    tchunk(3, cp)
-    tt(T.em[:, 0:8], T.stb[:, 8:16], T.stb[:, 0:8], A.is_le, "stb", "em")
-    ts(T.em[:, 8:16], T.em[:, 8:16], float(M + 1), A.add, "dj", "dj")
-    for c in range(6):
-        ts(T.l5[:, 8 * c:8 * c + 8], T.b0c[:], float(c if c < 5 else 264), A.add, "b0c", "l5%d" % c)
-        if c == 0:
-            tt(T.em[:, 16:24], T.em[:, 0:8], T.em[:, 8:16], A.mult, "em dj", "ed")
-        if c == 1:
-            tt(T.l2f[:, 0:8], T.em[:, 16:24], T.stb[:, 0:8], A.max, "ed stb", "l2a")
-            tt(T.l2f[:, 8:16], T.em[:, 16:24], T.stb[:, 8:16], A.max, "ed stb", "l2b")
-        if c == 2:
-            cp(T.l2[:], T.l2f[:], "l2a l2b", "l2")
-    D = T.pp[:, 256:384]
-    ts(wf[:, 0:128], D, T.bc[:, 0:1], A.is_le, "pp bc", "pa", BIG, A.mult)
-    ts(wf[:, 128:256], T.pp[:, 0:128], P16, A.is_gt, "pp pf", "pc", BIG, A.mult)
+    ts(T.tp[:, 0:256], T.tb[:], float(r * W), A.subtract, "tb", "tph")
+    ts(T.pfi[:, 0:256], T.tb[:], float(r * W), A.subtract, "tb", "pfi", n="tpf")
+    tt(T.tp[:, 256:512], T.pfi[:, 0:256], T.tp[:, 0:256], A.subtract, "pfi tph", "tpl")
+    dmas([("Dtw0", "y", T.tw[0::16, :], T.tp[:, 0:256], "tph", TW), ("Dtw1", "y", T.tw[1::16, :], T.tp[:, 256:512], "tpl", TW)])
+    cp(T.pmu[:], T.pmi[:], "pmi", "pmu")
+    for a, b, e in TCH:
+        move[e](T.tsw[:, a:b], T.tw[:].indirect(T.pmu[:, a // 16:b // 16]), TW + " pmu", keys("t", a, b), "T%d" % a)
+    for a in range(0, M, 1024):
+        b = a + 1024 + (128 if a == 3072 else 0)
+        mm("K%d" % a, spread(T.pk[:, a // 16:b // 16], T.z, T.tsw, a, b, True, True), "z pad " + keys("t", a, b), "pk:%d" % a)
+    for a, b in ((0, 124), (124, 191), (191, 258)):
+        mm("P%d" % a, [(T.pk2[:, a:b], T.z[:, 15 - k:143 - k], T.tsw[:, 16 * (a + k + 1):16 * (b + k) + 1:16], k == 0, k == 3)
+                       for k in range(4)], "z pad " + keys("t", 16 * (a + 1), 16 * (b + 3) + 1), "pk2:%d" % a)
+    cp(T.kwa[:], T.pk[:, 0:264], "pk:0 pk:1024 pk:2048 pk:3072", "kwa")
+    cp(T.kwb[:, 0:258], T.pk2[:, 0:258], "pk2:0 pk2:124 pk2:191", "kwb")
+    ts(T.sf[:], T.srow[:], 1.0 / 16, A.mult, "srow", "sf", -7.5 / 16, A.add)
+    lin(T.sx[:], T.sf[:], 1.0, RND, "sf", "sx")
+    lin(T.pq2[:, 0:128], T.sx[:, 0:128], 16.0, -16 * RND, "sx", "pq2", n="b16p")
+    lin(T.rd0[:, 256:384], T.sx[:, 0:128], 16.0, -16 * RND, "sx", "b16")
+    tt(T.rd0[:, 0:128], T.srow[:, 0:128], T.pq2[:, 0:128], A.subtract, "srow pq2", "rd0")
+    tt(T.rd0[:, 128:256], T.srow[:, 1:129], T.pq2[:, 0:128], A.subtract, "srow pq2", "rd1")
+    mm("bc", [(T.pp[:, 0:384], T.bb[:], T.rd0[:], True, False), (T.pp[:, 0:128], T.kn[0:1, :], T.one[0:1, :], False, False),
+              (T.pp[:, 128:256], T.kn[0:1, :], T.one[0:1, :], False, True)], "bb kn one rd0 rd1 b16", "pp")
+    lin(T.em[:, 0:8], ST, 1.0 / 16, -7.5 / 16, "qtr", "b0")
+    lin(T.em[:, 8:16], T.em[:, 0:8], 1.0, RND, "b0", "b0x")
+    for c in range(5):
+        lin(T.lf[:, 8 * c:8 * c + 8], T.em[:, 8:16], 1.0, c - RND, "b0x", "lf%d" % c)
+    tt(T.em[:, 16:24], EN, ST, A.is_le, "qtr", "em")
+    tt(T.em[:, 24:32], T.em[:, 16:24], T.dj[:], A.mult, "em dj", "ed")
+    tt(T.lf[:, 40:48], T.em[:, 24:32], ST, A.max, "ed qtr", "lf5")
+    tt(T.lf[:, 48:56], T.em[:, 24:32], EN, A.max, "ed qtr", "lf6")
+    cp(T.l5[:, 0:56], T.lf[:, 0:56], "lf0 lf1 lf2 lf3 lf4 lf5 lf6", "l5")
+    FIRST, END = T.l5[:, 40:48], T.l5[:, 48:56]
+    D = T.pp[:, 128:256]
+    lin(T.pa[:, 0:128], D, -BIG, BIG, "pp", "pa", F.Relu)
+    lin(T.pa[:, 128:256], T.pp[:, 0:128], BIG, 0.0, "pp", "pc", F.Relu)
+    tt(T.pen[:, 0:128], T.pa[:, 0:128], T.pa[:, 128:256], A.subtract, "pa pc", "pen0")
     for c in range(1, 5):
-        ts(T.pen[:, 128 * c:128 * (c + 1)], D, T.bc[:, c:c + 1], A.is_le, "pp bc", "pen%d" % c, BIG, A.mult)
-    ts(wf[:, 256:384], D, BA, A.is_le, "pp sa ba", "pd", SA, A.mult)
-    cp(T.bt[:], T.pp[:, 128:256], "pp", "bt")
-    tt(T.pen[:, 0:128], wf[:, 0:128], wf[:, 128:256], A.subtract, "pa pc", "pen0")
-    tchunk(1, act)
-    kchunk(1)
-    k2(0, 124, "ts0 ts1")
-    kchunk(3)
-    k2(191, 258, "ts3 tsp")
-    tchunk(2, act)
-    act(T.fs[:], T.tsw[:].indirect(T.l2[:, 0:8]), "ts0 ts1 ts2 ts3 tsp l2", "fs")
-    kchunk(2)
-    k2(124, 191, "ts1 ts2 ts3")
-    mm([(T.pfi[:, 0:128], T.z[:, 11:139], T.fs[:], True, True)], "z fs", "pfi")
-    wr["lqr"] = [("qa", arrive)]
-    cnt["qa"] = arrive
-    mm([(T.pq1[:, 0:384], T.b12[:], T.lq[:, 0:384], True, True)], "b12 lqo lqr", "pq1")
-    mm([(T.pq2[:, 0:384], T.b12[:], T.lq[:, 384:768], True, True)], "b12 lqo lqr", "pq2")
-    mm(spread(T.pi[:, 0:48], T.z0, T.lq, 0, 768, True, True), "z0 lqo lqr", "pi")
-    mm(spread(T.pb[:, 0:48], T.z0, T.lq, 0, 768, True, False), "z0 lqo lqr", "pb")
-
-    def xchunk(c):
-        act(T.xs[:, 1024 * c:1024 * (c + 1)], T.xw[:].indirect(T.pmu[:, 64 * c:64 * (c + 1)]), "xw pmu", "xs%d" % c)
-
-    def fill(a, b):
-        keys = " ".join("xs%d" % c for c in range(a // 1024, b // 1024))
-        ts(T.mk[:, a:b], T.xs[:, a:b], 0.0, A.is_equal, keys, "mk")
-        cp(T.mk[:].indirect(T.l2[:, 0:8]), T.cw[:, 0:128], "l2 cw0", "mk")
-        scan(T.ff[:, a + 1:b + 1], T.mk[:, a:b], T.xs[:, a:b], T.ff[:, a:a + 1] if a else 0.0, "mk ff " + keys, "ff")
-    xchunk(0)
+        lin(T.pen[:, 128 * c:128 * (c + 1)], D, -BIG, BIG * (16 * c + 1), "pp", "pen%d" % c, F.Relu)
+    tt(T.ta2[:], T.kwa[:].indirect(T.l5[:, 0:40]), T.pen[:], A.add, "kwa l5 pen0 pen1 pen2 pen3 pen4", "ta2")
+    cp(T.fs[:], T.tsw[:].indirect(FIRST), keys("t", 0, M) + " pad l5", "fs")
+    lin(T.pd[:], D, SA, BA, "pp ct ba", "pd", F.Relu)
+    lin(T.ub[:], T.pp[:, 256:384], SU, BU, "pp ct", "ub")
+    lin(T.nb[:], T.ub[:], -1.0, 0.0, "ub", "nb")
+    mm("pfi", [(T.pfi[:, 0:128], T.eye[:], T.pd[:], True, False), (T.pfi[:, 0:128], T.eye[:], T.nb[:], False, False),
+               (T.pfi[:, 0:128], T.z[:, 11:139], T.fs[:], False, True)], "eye pd nb z fs", "pfi")
+    tt(T.pen5[:], T.pfi[:, 0:128], T.ub[:], A.add, "pfi ub", "pen5")
+    tt(T.ta1[:], T.kwb[:, 0:258].indirect(T.l5[:, 0:8]), T.pen5[:], A.add, "kwb l5 pen5", "ta1")
+    mm("q1", [(T.pq1[:, 0:384], T.b12[:], T.u[:, 0:384], True, True)], "b12 sw lqr", "pq1")
+    mm("q2", [(T.pq2[:, 0:384], T.b12[:], T.u[:, 384:768], True, True)], "b12 sw lqr", "pq2")
     act(T.qw[:, 0:384], T.pq1[:, 0:384], "pq1", "qw0")
     act(T.qw[:, 384:768], T.pq2[:, 0:384], "pq2", "qw1")
-    xchunk(1)
-    cp(T.kw[:, 0:264], T.pk[:, 0:264], "pk", "kwa")
-    cp(T.kw[:, 264:522], T.pk2[:, 0:258], "pk2", "kwb")
-    tt(T.pen[:, 640:768], T.pfi[:, 0:128], wf[:, 256:384], A.add, "pfi pd", "pen5")
-    tt(T.ta[:], T.kw[:, 0:522].indirect(T.l5[:]), T.pen[:], A.add,
-       "kwa kwb l50 l51 l52 l53 l54 l55 pen0 pen1 pen2 pen3 pen4 pen5", "ta")
+    mm("pi", spread(T.pi[:, 0:48], T.z0, T.u, 0, 768, True, True), "z0 sw lqr", "pi")
     cp(T.offa[:], T.pi[:, 0:48], "pi", "offa")
-    tt(T.ca[:], T.ta[:, 640:768].indirect(T.offa[:]), T.qw[:], A.is_le, "ta offa qw0 qw1", "ca")
-    xchunk(2)
-    xchunk(3)
-    act(T.gb[:], T.bt[:].indirect(T.offa[:]), "bt offa", "gb")
-    mm(spread(T.pb[:, 0:48], T.za1, T.ca, 0, 768, False, True), "za1 ca", "pb")
-    mm(spread(T.pp[:, 0:48], T.za2, T.ca, 0, 768, True, False), "za2 ca", "pp")
-    fill(0, 2048)
-    fill(2048, M)
+    lin(T.offab[:], T.pi[:, 0:48], 1.0 / 128, 0.0, "pi", "offab")
+    tt(T.ca[:], T.ta1[:].indirect(T.offa[:]), T.qw[:], A.is_le, "ta1 offa qw0 qw1", "ca")
+    mm("pb", [(T.pb[:, 0:48], T.eye[:], T.offab[:], True, False)] + spread(T.pb[:, 0:48], T.za1, T.ca, 0, 768, False, True),
+       "eye offab za1 ca", "pb")
+    mm("pp1", spread(T.pp[:, 0:48], T.za2, T.ca, 0, 768, True, False), "za2 ca", "pp")
+    ts(T.offb[:], T.pb[:, 0:48], 128.0, A.mult, "pb", "offb")
+    tt(T.cb[:], T.ta2[:].indirect(T.offb[:]), T.qw[:], A.is_le, "ta2 offb qw0 qw1", "cb")
+    mm("pp2", spread(T.pp[:, 0:48], T.z, T.cb, 0, 768, False, True), "z cb", "pp")
+    ts(T.offf[:], T.pp[:, 0:48], 8192.0, A.add, "pp", "offf", float(M + 1), A.min)
+    for a, b, e in XCH:
+        move[e](T.xs[:, a:b], T.xw[:].indirect(T.pmu[:, a // 16:b // 16]), "xwa xwb pmu", keys("x", a, b), "X%d" % a)
+    for a, b in FCH:
+        for c, d in MCH:
+            if a <= c < b:
+                ts(T.mk[:, c:d], T.xs[:, c:d], 0.0, A.is_equal, keys("x", c, d), keys("m", c, d), n="M%d" % c)
+        cp(T.mk[:].indirect(FIRST), T.zero[:], "l5 zero", keys("m", 0, M), "R%d" % a)
+        scan(T.ff[:, a + 1:b + 1], T.mk[:, a:b], T.xs[:, a:b], T.ff[:, a:a + 1] if a else 0.0,
+             "ff " + keys("m", a, b) + " " + keys("x", a, b), "ff", "F%d" % a)
     fw = T.ff[:]
 
     def last(s):
-        return T.cw[:, 128:256] if s == 0 else T.ll[:, 128 * s:128 * s + 128]
+        return T.lo[:] if s == r else T.ll[:, 128 * s:128 * s + 128]
     if r < N - 1:
-        cp(last(r), fw.indirect(T.l2[:, 8:16]), "ff ffp l2", "lol")
-        deps("g", ["lol"], [])
+        act(T.lo[:], fw.indirect(END), "ff ffp l5", "lo")
         to = [DstId(rid=topo.addr(cores[p])[0], pnc=topo.addr(cores[p])[1]) for p in peers]
-        g.remote_dma_fused([RemoteDMATransfer(dst_ids=to, dma_engine_mask=sum(1 << e for e in common(r)), remote_sem=T.sem.la,
-                                              src=last(r), dsts=[last(r)] * len(peers))], local_sem=T.sem.loc)
-        cnt["loc"] += len(common(r))
-    cp(T.offb[:], T.pb[:, 0:48], "pb", "offb")
-    tt(T.cb[:], T.ta[:, 0:640].indirect(T.offb[:]), T.qw[:], A.is_le, "ta offb qw0 qw1", "cb")
-    mm(spread(T.pp[:, 0:48], T.z0, T.gb, 0, 768, False, False), "z0 gb", "pp")
-    mm(spread(T.pp[:, 0:48], T.z, T.cb, 0, 768, False, True), "z cb", "pp")
-    lin(T.slf[:, 32:64], T.qtr[:, 32:64], 128.0, 0.0, "qtr", "s128")
-    tt(T.slf[:, 64:96], T.slf[:, 32:64], T.qtr[:, 0:32], A.add, "qtr s128", "cof")
-    cp(T.coff[:], T.slf[:, 64:96], "cof", "coff")
-    ts(T.offf[:], T.pp[:, 0:48], 8192.0, A.add, "pp", "offf", float(M + 1), A.min)
-
+        tr = RemoteDMATransfer(dst_ids=to, dma_engine_mask=sum(1 << e for e in common(r)), remote_sem=T.sem.la,
+                               src=T.lo[:], dsts=[T.ll[:, 128 * r:128 * r + 128]] * len(peers))
+        step("L", "g", lambda: g.remote_dma_fused([tr], local_sem=T.sem.loc), "lo", "", None)
+        total["loc"] += len(common(r))
+    for n in range(N):
+        move["vs"[n % 2]](blk(T.a, n), fw.indirect(T.offf[:, 12 * n:12 * n + 12]), "ff ffp offf", "oa%d" % n)
     for n, p in enumerate(peers):
-        (cp if n == 1 else act)(T.ob[:, CAP * p:CAP * (p + 1)], fw.indirect(T.offf[:, 12 * p:12 * p + 12]), "ff ffp offf", "oa%d" % p)
-        send(p, T.land[:, CAP * r:CAP * (r + 1)], T.ob[:, CAP * p:CAP * (p + 1)], "ra", "oa%d" % p)
-    cp(T.land[:, CAP * r:CAP * (r + 1)], fw.indirect(T.offf[:, 12 * r:12 * r + 12]), "ff ffp offf", "loa")
-    cnt["la"] = sum(len(common(p)) for p in peers if p < N - 1)
-    wr["llr"] = [("la", cnt["la"])]
-    LK = "llr lol"
-    ts(T.m1[:], T.ll[:, 128:384], 0.0, A.is_equal, LK, "m1")
-    tt(T.c1[:, 0:128], T.m1[:, 0:128], last(0), A.mult, LK + " m1", "c1")
-    tt(T.cw[:, 256:384], T.c1[:, 0:128], last(1), A.add, LK + " c1", "cw2")
-    tt(T.c1[:, 128:256], T.m1[:, 128:256], T.cw[:, 256:384], A.mult, "m1 cw2", "c2")
-    tt(T.cw[:, 384:512], T.c1[:, 128:256], last(2), A.add, LK + " c2", "cw3")
-    cp(T.cz[:], T.cw[:].indirect(T.coff[:]), LK + " cw0 cw2 cw3 coff", "cg")
-    cp(T.pk[:], T.cz[:], "cg", "pk")
-    wr["lar"] = [("ra", arrive)]
-    cnt["ra"] = arrive
-    pv = (T.pq1[:, 0:256], T.pq2[:, 0:256])
+        send("A%d" % n, p, blk(T.a, 4 + peers_of(p).index(r)), blk(T.a, n), "ra", "oa%d" % n)
+
+    lin(T.slf[:, 32:64], QI, 4.0, 0.0, "qtr", "qi4")
+    tt(T.slf[:, 64:96], T.slf[:, 32:64], SI, A.add, "qtr qi4", "cof")
+    cp(T.coff[:], T.slf[:, 64:96], "cof", "coff")
+    for s in range(N - 1):
+        k = "lo" if s == r else "llr"
+        if s:
+            ts(T.zl[:, s + 1::4], last(s), 0.0, A.is_equal, k, "zl%d" % (s + 1))
+        (cp if s == 0 else act)(T.il[:, s + 1::4], last(s), k, "il%d" % (s + 1))
+    scan(T.cw[:], T.zl[:], T.il[:], 0.0, "il0 il1 il2 il3 zl zl2 zl3", "cw")
     for h in range(2):
-        c = slice(256 * h, 256 * (h + 1))
-        win = T.land[:].indirect(T.slot[:, 16 * h:16 * (h + 1)])
-        act(T.v[:, c], win, "lar loa slot", "v%d" % h)
-        mm([(pv[h], T.eye[:], T.v[:, c], True, h == 1)], "eye v%d" % h, "pq%d" % (h + 1))
-        ts(T.mv[:, c], win, 0.0, A.is_equal, "lar loa slot", "mv%d" % h)
-        tt(T.cz[:, c], T.pk[:, c], T.mv[:, c], A.mult, "pk cg mv%d" % h, "cz%d" % h)
-    mm([(pv[0], T.eye[:], T.cz[:, 0:256], False, True)], "eye cz0", "pq1")
-    act(T.yo[:, 0:256], pv[0], "pq1", "yo0")
-    dmas([("s", T.y[:, 0:256], T.yo[:, 0:256], "yo0", "")])
-    tt(T.yo[:, 256:512], pv[1], T.cz[:, 256:512], A.add, "pq2 cz1", "yo1")
-    dmas([("y", T.y[:, 256:512], T.yo[:, 256:512], "yo1", "")])
-    for s in cnt:
-        wait("g", (s, cnt[s]))
+        c = slice(512 * h, 512 * (h + 1))
+        odd = slice(512 * h + 1, 512 * (h + 1), 2)
+        move["sv"[h]](T.iv[:, 512 * h:512 * (h + 1):2], T.cw[:].indirect(T.coff[:, 16 * h:16 * (h + 1)]), "cw coff", "cz%d" % h)
+        move["sv"[h]](T.iv[:, odd], T.a[:, 576:1344].indirect(T.slot[:, 16 * h:16 * (h + 1)]), "lar oa3 slot", "v%d" % h)
+        ts(T.zv[:, odd], T.iv[:, odd], 0.0, A.is_equal, "zv v%d" % h, "zv%d" % h)
+        scan(T.ov[:, c], T.zv[:, c], T.iv[:, c], 0.0, "zv zv%d v%d cz%d" % (h, h, h), "ov%d" % h)
+        move["vs"[h]](T.yo[:, 256 * h:256 * (h + 1)], T.ov[:, odd], "ov%d" % h, "yo%d" % h)
+        dmas([("Y%d" % h, "ys"[h], T.y[:, 256 * h:256 * (h + 1)], T.yo[:, 256 * h:256 * (h + 1)], "yo%d" % h, "")])
+
+    todo = {e: [n for n in ORDER[e].split() if n in steps] for e in ORDER}
+    assert sorted(n for e in todo for n in todo[e]) == sorted(steps) and all(steps[n][0] == e for e in todo for n in todo[e])
+    done, seen = {s: (s, total[s]) for s in ("qa", "la", "ra")}, {}
+    group = {s: [n for n in steps if steps[n][2] == s] for s in total}
+
+    def wait(e, s, v):
+        if seen.get((e, s), 0) < v:
+            qs[e].wait_ge(T.sem[s], v)
+            seen[(e, s)] = v
+
+    def ready(n):
+        return all(m in done for t in steps[n][3] for m in (group.get(steps[t][2], [t]) if t in steps else [t]))
+    while any(todo.values()):
+        e = [e for e in todo if todo[e] and ready(todo[e][0])][0]
+        n = todo[e].pop(0)
+        fn, s, dep = steps[n][1:]
+        need = {}
+        for t in dep:
+            need[done[t][0]] = max(need.get(done[t][0], 0), done[t][1])
+        for t in sorted(need):
+            wait(e, t, need[t])
+        call = fn()
+        if s in esem.values():
+            total[s] = total.get(s, 0) + 1
+        if s:
+            call.then_inc(T.sem[s], 1 if s in esem.values() else 16)
+        done[n] = (s, total.get(s))
+    for s in total:
+        wait("g", s, total[s])

@@ -8,32 +8,38 @@ RND = 1.5 * 2 ** 23
 BF, F32, I32, U16 = "bfloat16", "float32", "int32", "uint16"
 COLS = {
     BF: dict(one=128, kn=128, bb=128, b12=128, lin=128, eye=128, z=144, z0=144, za1=144, za2=144, pcs=96, oh=136, rst=136,
-             sc=136, rows=512, u=1344, tp=512, tw=M, tsw=PAD, rd0=384, nb=128, pen=640, pa=256, pd=128, fs=128, xw=M, xs=M,
+             sc=136, rows=512, u=1344, tp=512, tw=M, tsw=PAD, nb0=128, nb=128, pen=640, pa=256, pd=128, fs=128, xw=M, xs=M,
              mk=PAD, ff=PAD, ca=768, cb=768, a=1344, lo=128, ll=384, il=512, zl=512, cw=512, iv=1024, zv=1024,
-             ov=1024, yo=512, zero=128, offab=48),
-    F32: dict(pf=8, c0=32, cd=128, cr=160, ct=160, qf=96, qtr=96, prod=136, t1=72, slf=96, sf=136, sx=136, dj=8, em=32, lf=64,
-              ub=128, kwa=264, kwb=264, pen5=128, ta1=128, ta2=640, qw=768),
+             ov=1024, yo=512, zero=128, ul=96),
+    F32: dict(pf=8, c0=32, cd=128, cr=160, ct=160, qf=96, qtr=96, prod=136, t1=72, slf=96, sf=136, sx=128, dj=8, em=32, lf=64,
+              bbf=128, ub=128, kwa=264, kwb=264, pen5=128, ta1=128, ta2=640, qw=768, g2=768),
     I32: dict(qp=128, qn=32, qm=96, tb=256, pmi=256, srow=136),
     U16: dict(slot=32, coff=32, pmu=256, l5=64, offa=48, offb=48, offf=48),
 }
 PS = ("pk", "pk2", "pq1", "pq2", "pb", "pp", "pi", "pfi")
 SCRATCH = {n: ("sbuf", [128, c], d) for d in COLS for n, c in COLS[d].items()}
 SCRATCH.update({n: ("psum", [128, 512], F32) for n in PS})
-SEMAPHORES = ["ev", "es", "et", "eg", "qa", "la", "ra", "loc"] + ["d%d" % k for k in range(20)]
+SEMAPHORES = ["ev", "es", "et", "eg", "qa", "ia", "la", "ra", "loc"] + ["d%d" % k for k in range(20)]
 XA = 512
 TCH = ((0, 1024, "s"), (1024, 2048, "s"), (2048, 2816, "s"), (3072, M, "v"), (2816, 3072, "v"))
-XCH = ((0, 512, "s"), (512, 1024, "s"), (1024, 2048, "s"), (2048, 3072, "s"), (3072, 3584, "v"), (3584, M, "s"))
-MCH = ((0, 1024), (1024, 2048), (2048, M))
-FCH = ((0, M),)
+XCH = ((0, 512, "s"), (512, 1024, "s"), (1024, 2048, "s"), (2048, 3072, "s"), (3072, 3584, "v"), (3584, M, "v"))
+MCH = ((0, 1024), (1024, 2048), (2048, 3072), (3072, 3584), (3584, M))
+FCH = ((0, 3072), (3072, M))
+CZ = "sv"
+VV = "sv"
+QC = ((0,), (1,), (2,))
+IC = ((0, 1, 2),)
+AC = ((0,), (1,), (2,))
 ORDER = dict(
-    y="Ltb Lst0 Lst1 Lst2 Lst3 Lsrow Lpm Dtw0 Dtw1 Drow0 Drow1 Drow2 Lxa Lxb Y0",
-    s="Lqt0 Lqt1 Lqi0 Lqi1 Lqn Lqm tw0 tw1 tw2 tw3 rst sw sw2 rst0 sx b0 b16p b16 b0x T0 T1024 T2048 lf0 lf1 lf2 lf3 lf4 "
-      "ba ub pa pc pd nb pen1 pen2 pen3 pen4 X0 X512 qw0 qw1 offab X1024 X2048 X3584 qi4 lo oa1 oa3 il2 il3 cz0 v0 yo1 Y1",
-    v="st rows srow tw4 tph tpf si tpl low hi qf sf qtr pcs oh0 oh1 oh2 oh3 sc pmu rd0 prod rd1 t1 em slf ed slot pad scat "
-      "lf5 T3072 cr0 lf6 ct T2816 X3072 l5 fs pen0 kwa kwb pen5 ta2 ta1 offa ca M0 za2 M1024 offb cb M2048 cof R0 coff F0 offf "
-      "oa0 oa2 zl2 il1 zl3 cw cz1 v1 zv1 zv0 ov1 ov0 yo0",
-    t="slotm bc K0 K1024 P0 K3072 P191 K2048 P124 pfi q1 q2 pi pb pp1 pp2",
-    g="one bb0 bb ohl lin dj z zs kn c0 cd0 cd1 cd2 cd3 cd4 cr1 cr2 cr3 Q0 Q1 Q2 eye b12 z0 za1 zero ffp ff il0 zl zv L A0 A1 A2",
+    y="Ltb Lst0 Lst1 Lst2 Lst3 Lpm Lsrow Dtw0 Dtw1 Drow0 Drow1 Drow2 Lxa Lxb Y0",
+    s="Lqt0 Lqt1 Lqn Lqm Lqi0 Lqi1 tw0 tw1 tw2 tw3 tph bbf rst sw rst0 b0 b0x sx lf0 lf1 lf2 lf3 lf4 b16 T0 T2048 T1024 "
+      "ba pc ub ul pa pd nb pen1 pen2 pen3 pen4 X0 X512 qw0 qw1 X2048 X1024 za2 g20 g21 lo oa1 qi4 oa3 il2 il3 cz0 v0 yo1 Y1",
+    v="st rows sw2 srow tw4 tpf low hi si pcs qf tpl qtr sf oh0 oh1 oh2 oh3 em sc ed pmu prod lf6 t1 lf5 slf l5 slot scat "
+      "cr0 T3072 ct T2816 X3072 kwb fs X3584 pen5 pen0 M3584 ta1 M3072 offa M0 ca kwa M2048 ta2 offb M1024 R0 cb0 F0 cb1 F3072 offf "
+      "oa0 oa2 cof coff zl2 il1 zl3 cw cz1 v1 zv1 zv0 ov1 ov0 yo0",
+    t="bc0 slotm bc K0 pi P191 P0 P124 K3072 pfi q1 q2 K1024 K2048 pb pp1 pp2",
+    g="one z c0 ohl bb0 bb dj lin kn zs cd0 cd1 cd2 cd3 pad cd4 cr1 cr2 cr3 z0 Q0 Q1 Q2 I0 eye b12 zero za1 zl il0 zv ffp ff "
+      "L A0 A1 A2",
 )
 
 
@@ -119,30 +125,45 @@ def rank_program(g, core, T, topo):
     def peers_of(a):
         def far(p):
             x, y = topo.chip(cores[a]), topo.chip(cores[p])
-            return 2 if x == y else 1 if topo.mates(x, y) or topo.same_plane(x, y) else 0
+            return 3 if x == y else 2 if topo.mates(x, y) else 1 if topo.same_plane(x, y) else 0
         return sorted([p for p in range(N) if p != a], key=far)
     peers = peers_of(r)
-
-    def width(a, b):
-        return len(topo.engines(cores[a], cores[b]))
 
     def common(a):
         return [e for e in topo.engines(cores[a], cores[(a + 1) % N])
                 if all(e in topo.engines(cores[a], cores[b]) for b in range(N) if b != a)]
 
-    def send(n, p, dst, src, sem, R):
-        rid, pid, se = topo.addr(cores[p])
-        step(n, "g", lambda: g.remote_dma(dst, src, T.sem[sem], T.sem.loc, pid, rid, topo.mask(core, cores[p])), R, "", None)
-        total["loc"] += width(r, p)
+    def shares(a, call):
+        es, out = common(a), []
+        for k in range(len(call)):
+            n = len(es) if k == len(call) - 1 else len(es) // 2
+            out.append(es[:n])
+            es = es[n:]
+        return out
+
+    def send(name, calls, sem, part):
+        for call in calls:
+            trs = []
+            for n, es in zip(call, shares(r, call)):
+                rid, pid, se = topo.addr(cores[peers[n]])
+                trs.append(RemoteDMATransfer(dst_ids=[DstId(rid=rid, pnc=pid)], dma_engine_mask=sum(1 << e for e in es),
+                                             remote_sem=T.sem[sem], src=part(n)[1], dst=part(n)[0]))
+            step("%s%d" % (name, call[0]), "g", lambda trs=trs: g.remote_dma_fused(trs, local_sem=T.sem.loc),
+                 " ".join(part(n)[2] for n in call), "", None)
+            total["loc"] += len(common(r))
+        total[sem] = sum(len(es) for p in peers for call in calls for n, es in zip(call, shares(p, call)) if peers_of(p)[n] == r)
+
+    def there(n):
+        return peers_of(peers[n]).index(r)
 
     def blk(t, n):
         return t[:, CAP * n:CAP * (n + 1)]
 
     def keys(n, a, b):
         return " ".join("%s.%d" % (n, c) for c in range(a // 256, (b + 255) // 256))
-    total["qa"] = total["ra"] = sum(width(p, r) for p in peers)
+    total.update(qa=0, ia=0, ra=0)
     total["la"] = sum(len(common(p)) for p in peers if p < N - 1)
-    wr.update(lqr=["qa"], llr=["la"], lar=["ra"])
+    wr.update(lqr=["qa"], lqi=["ia"], llr=["la"], lar=["ra"])
 
     ms(T.qp[:, 64:96], 0, "st")
     ms(T.srow[:], 0, "srow")
@@ -164,8 +185,8 @@ def rank_program(g, core, T, topo):
     TW = "tw0 tw1 tw2 tw3 tw4"
     lin(T.rst[:], T.rows[:, 0:136], 0.0, 1.0, "rows", "rst")
     act(T.u[:, 576:960], T.rows[:, 0:384], "rows", "sw")
-    act(T.u[:, 960:1344], T.rows[:, 0:384], "rows", "sw2")
-    ms(T.tsw[:, M:PAD], float(W), "pad")
+    ms(T.u[:, 960:1344], 0.0, "sw2")
+    iota(T.tsw[:, M:PAD], [[0, PAD - M]], W, "pad")
     iota(T.one[:], [[0, 128]], 1, "one")
     sel(T.bb[:], T.one[:], [[-16, 8], [0, 16]], A.is_ge, 0, 1, "one", "bb", n="bb0")
     sel(T.bb[:], T.bb[:], [[16, 8], [0, 16]], A.is_ge, 15, -1, "bb", "bb")
@@ -174,7 +195,7 @@ def rank_program(g, core, T, topo):
     lin(T.rst[:, 0:132:33], T.oh[:, 0:132:33], 0.0, 0.0, "ohl", "rst", n="rst0")
     iota(T.z[:], [[0, 144]], 0, "z")
     sel(T.z[:, 15:143:16], T.bb[:, 0::16], [[0, 8]], A.is_ge, 0, 0, "bb", "z", n="zs")
-    iota(T.kn[0:1, :], [[0, 8], [-1, 16]], 0, "kn")
+    iota(T.kn[0:1, :], [[0, 8], [-1, 16]], 7, "kn")
     iota(T.dj[:], [[16, 8]], M + 1, "dj", 1)
     sel(T.b12[:], T.bb[:], [[-16, 8], [0, 16]], A.not_equal, 0, 1, "bb", "b12")
     sel(T.z0[:], T.z[:], [[1, 144]], A.is_equal, -15, -1, "z", "z0")
@@ -191,7 +212,7 @@ def rank_program(g, core, T, topo):
     sel(T.cd[:, 0:32], T.c0[:], KN, A.is_ge, 5, 0, "c0", "cd0", 2.0)
     sel(T.cd[:, 32:64], T.c0[:], KN, A.is_ge, 5, 0, "c0", "cd1", 0.5)
     sel(T.cd[:, 64:96], T.c0[:], K, A.is_ge, -6, 0, "c0", "cd2", 16.0)
-    sel(T.cd[:, 96:128], T.c0[:], K, A.not_equal, -5, 0, "c0", "cd3", 2.0 ** 23)
+    sel(T.cd[:, 96:128], T.c0[:], K, A.not_equal, -5, 0, "c0", "cd3", -2.0 ** 27)
     sel(T.cd[:, 64:96], T.cd[:, 64:96], K, A.not_equal, -4, 0, "cd2", "cd2", -8192.0, "cd4")
     sel(T.cr[:, 64:96], T.c0[:], KN, A.is_ge, 4, 0, "c0", "cr1", 2.0 ** 35 + 2.0 ** 17)
     sel(T.cr[:, 96:128], T.c0[:], K, A.is_ge, -4, 0, "c0", "cr2", -BIG)
@@ -201,7 +222,7 @@ def rank_program(g, core, T, topo):
     WA2, SU, BU, SA, N17 = [T.ct[:, 32 * k:32 * k + 1] for k in range(5)]
     BA = T.pf[:, 0:1]
     lin(BA, N17, SA, 0.0, "ct", "ba")
-    ts(T.za2[:], T.z[:], WA2, A.mult, "z ct", "za2")
+    lin(T.za2[:], T.z[:], WA2, 0.0, "z ct", "za2")
 
     ts(T.qp[:, 96:128], T.qp[:, 0:32], 16, A.arith_shift_right, "qt", "si")
     ts(T.qm[:, 32:64], T.qn[:], 0xFF00, A.bitwise_and, "qn", "hi")
@@ -222,11 +243,13 @@ def rank_program(g, core, T, topo):
     tt(T.slf[:, 0:32], T.t1[:, 0:32], T.t1[:, 33:65], A.add, "t1", "slf")
     cp(T.slot[:], T.slf[:, 0:32], "slf", "slot")
     cp(T.u[:, 576:1344].indirect(T.slot[:]), T.rows[:], "slot rows", "sw sw2", "scat")
-    for n, p in enumerate(peers):
-        send("Q%d" % n, p, blk(T.u, peers_of(p).index(r)), blk(T.u, 4 + n), "qa", "sw")
+    send("Q", QC, "qa", lambda n: (blk(T.u, there(n)), blk(T.u, 4 + n), "sw"))
+    mm("pi", spread(T.pi[:, 0:48], T.z0, T.u, 576, 1344, True, True), "z0 sw sw2", "pi")
+    lin(T.ul[:, 40:88], T.pi[:, 0:48], 1.0 / 128, 0.0, "pi", "ul")
+    send("I", IC, "ia", lambda n: (T.ul[:, 4 + 12 * there(n):16 + 12 * there(n)], T.ul[:, 52 + 12 * n:64 + 12 * n], "ul"))
 
-    ts(T.tp[:, 0:256], T.tb[:], float(r * W), A.subtract, "tb", "tph")
     ts(T.pfi[:, 0:256], T.tb[:], float(r * W), A.subtract, "tb", "pfi", n="tpf")
+    act(T.tp[:, 0:256], T.pfi[:, 0:256], "pfi", "tph")
     tt(T.tp[:, 256:512], T.pfi[:, 0:256], T.tp[:, 0:256], A.subtract, "pfi tph", "tpl")
     dmas([("Dtw0", "y", T.tw[0::16, :], T.tp[:, 0:256], "tph", TW), ("Dtw1", "y", T.tw[1::16, :], T.tp[:, 256:512], "tpl", TW)])
     cp(T.pmu[:], T.pmi[:], "pmi", "pmu")
@@ -240,14 +263,15 @@ def rank_program(g, core, T, topo):
                        for k in range(4)], "z pad " + keys("t", 16 * (a + 1), 16 * (b + 3) + 1), "pk2:%d" % a)
     cp(T.kwa[:], T.pk[:, 0:264], "pk:0 pk:1024 pk:2048 pk:3072", "kwa")
     cp(T.kwb[:, 0:258], T.pk2[:, 0:258], "pk2:0 pk2:124 pk2:191", "kwb")
-    ts(T.sf[:], T.srow[:], 1.0 / 16, A.mult, "srow", "sf", -7.5 / 16, A.add)
-    lin(T.sx[:], T.sf[:], 1.0, RND, "sf", "sx")
-    lin(T.pq2[:, 0:128], T.sx[:, 0:128], 16.0, -16 * RND, "sx", "pq2", n="b16p")
-    lin(T.rd0[:, 256:384], T.sx[:, 0:128], 16.0, -16 * RND, "sx", "b16")
-    tt(T.rd0[:, 0:128], T.srow[:, 0:128], T.pq2[:, 0:128], A.subtract, "srow pq2", "rd0")
-    tt(T.rd0[:, 128:256], T.srow[:, 1:129], T.pq2[:, 0:128], A.subtract, "srow pq2", "rd1")
-    mm("bc", [(T.pp[:, 0:384], T.bb[:], T.rd0[:], True, False), (T.pp[:, 0:128], T.kn[0:1, :], T.one[0:1, :], False, False),
-              (T.pp[:, 128:256], T.kn[0:1, :], T.one[0:1, :], False, True)], "bb kn one rd0 rd1 b16", "pp")
+    ts(T.sf[:], T.srow[:], 7.0 / 16, A.subtract, "srow", "sf")
+    act(T.bbf[:], T.bb[:], "bb", "bbf")
+    mm("bc0", [(T.pq2[:, 0:128], T.bbf[:], T.sf[:, 0:128], True, True)], "bbf sf", "pq2")
+    lin(T.sx[:], T.pq2[:, 0:128], (1 - 2.0 ** -13) / 16, RND, "pq2", "sx")
+    lin(T.nb0[:], T.sx[:], -1.0, RND, "sx", "b16")
+    mm("bc", [c for h in range(2) for c in ((T.pp[:, 128 * h:128 * h + 128], T.bbf[:], T.sf[:, h:128 + h], True, False),
+                                            (T.pp[:, 128 * h:128 * h + 128], T.bb[:], T.nb0[:], False, False),
+                                            (T.pp[:, 128 * h:128 * h + 128], T.kn[0:1, :], T.one[0:1, :], False, True))],
+       "bb bbf kn one sf b16", "pp")
     lin(T.em[:, 0:8], ST, 1.0 / 16, -7.5 / 16, "qtr", "b0")
     lin(T.em[:, 8:16], T.em[:, 0:8], 1.0, RND, "b0", "b0x")
     for c in range(5):
@@ -259,15 +283,15 @@ def rank_program(g, core, T, topo):
     cp(T.l5[:, 0:56], T.lf[:, 0:56], "lf0 lf1 lf2 lf3 lf4 lf5 lf6", "l5")
     FIRST, END = T.l5[:, 40:48], T.l5[:, 48:56]
     D = T.pp[:, 128:256]
-    lin(T.pa[:, 0:128], D, -BIG, BIG, "pp", "pa", F.Relu)
+    lin(T.pb[:, 0:128], D, -BIG, BIG, "pp", "pb", F.Relu, "pa")
     lin(T.pa[:, 128:256], T.pp[:, 0:128], BIG, 0.0, "pp", "pc", F.Relu)
-    tt(T.pen[:, 0:128], T.pa[:, 0:128], T.pa[:, 128:256], A.subtract, "pa pc", "pen0")
+    tt(T.pen[:, 0:128], T.pb[:, 0:128], T.pa[:, 128:256], A.subtract, "pb pc", "pen0")
     for c in range(1, 5):
         lin(T.pen[:, 128 * c:128 * (c + 1)], D, -BIG, BIG * (16 * c + 1), "pp", "pen%d" % c, F.Relu)
     tt(T.ta2[:], T.kwa[:].indirect(T.l5[:, 0:40]), T.pen[:], A.add, "kwa l5 pen0 pen1 pen2 pen3 pen4", "ta2")
     cp(T.fs[:], T.tsw[:].indirect(FIRST), keys("t", 0, M) + " pad l5", "fs")
     lin(T.pd[:], D, SA, BA, "pp ct ba", "pd", F.Relu)
-    lin(T.ub[:], T.pp[:, 256:384], SU, BU, "pp ct", "ub")
+    lin(T.ub[:], T.nb0[:], SU, BU, "b16 ct", "ub")
     lin(T.nb[:], T.ub[:], -1.0, 0.0, "ub", "nb")
     mm("pfi", [(T.pfi[:, 0:128], T.eye[:], T.pd[:], True, False), (T.pfi[:, 0:128], T.eye[:], T.nb[:], False, False),
                (T.pfi[:, 0:128], T.z[:, 11:139], T.fs[:], False, True)], "eye pd nb z fs", "pfi")
@@ -277,24 +301,24 @@ def rank_program(g, core, T, topo):
     mm("q2", [(T.pq2[:, 0:384], T.b12[:], T.u[:, 384:768], True, True)], "b12 sw lqr", "pq2")
     act(T.qw[:, 0:384], T.pq1[:, 0:384], "pq1", "qw0")
     act(T.qw[:, 384:768], T.pq2[:, 0:384], "pq2", "qw1")
-    mm("pi", spread(T.pi[:, 0:48], T.z0, T.u, 0, 768, True, True), "z0 sw lqr", "pi")
-    cp(T.offa[:], T.pi[:, 0:48], "pi", "offa")
-    lin(T.offab[:], T.pi[:, 0:48], 1.0 / 128, 0.0, "pi", "offab")
+    ts(T.offa[:], T.ul[:, 4:52], 128.0, A.mult, "ul lqi", "offa")
     tt(T.ca[:], T.ta1[:].indirect(T.offa[:]), T.qw[:], A.is_le, "ta1 offa qw0 qw1", "ca")
-    mm("pb", [(T.pb[:, 0:48], T.eye[:], T.offab[:], True, False)] + spread(T.pb[:, 0:48], T.za1, T.ca, 0, 768, False, True),
-       "eye offab za1 ca", "pb")
+    mm("pb", [(T.pb[:, 0:48], T.eye[:], T.ul[:, 4:52], True, False)] + spread(T.pb[:, 0:48], T.za1, T.ca, 0, 768, False, True),
+       "eye ul lqi za1 ca", "pb")
     mm("pp1", spread(T.pp[:, 0:48], T.za2, T.ca, 0, 768, True, False), "za2 ca", "pp")
     ts(T.offb[:], T.pb[:, 0:48], 128.0, A.mult, "pb", "offb")
-    tt(T.cb[:], T.ta2[:].indirect(T.offb[:]), T.qw[:], A.is_le, "ta2 offb qw0 qw1", "cb")
-    mm("pp2", spread(T.pp[:, 0:48], T.z, T.cb, 0, 768, False, True), "z cb", "pp")
+    for h in range(2):
+        c = slice(384 * h, 384 * h + 384)
+        act(T.g2[:, c], T.ta2[:].indirect(T.offb[:, 24 * h:24 * h + 24]), "ta2 offb", "g2%d" % h)
+        tt(T.cb[:, c], T.g2[:, c], (T.pq1, T.pq2)[h][:, 0:384], A.is_le, "g2%d pq%d" % (h, h + 1), "cb%d" % h)
+    mm("pp2", spread(T.pp[:, 0:48], T.z, T.cb, 0, 768, False, True), "z cb0 cb1", "pp")
     ts(T.offf[:], T.pp[:, 0:48], 8192.0, A.add, "pp", "offf", float(M + 1), A.min)
     for a, b, e in XCH:
         move[e](T.xs[:, a:b], T.xw[:].indirect(T.pmu[:, a // 16:b // 16]), "xwa xwb pmu", keys("x", a, b), "X%d" % a)
+    for c, d in MCH:
+        ts(T.mk[:, c:d], T.xs[:, c:d], 0.0, A.is_equal, keys("x", c, d), keys("m", c, d), n="M%d" % c)
+    cp(T.mk[:].indirect(FIRST), T.zero[:], "l5 zero", keys("m", 0, M), "R0")
     for a, b in FCH:
-        for c, d in MCH:
-            if a <= c < b:
-                ts(T.mk[:, c:d], T.xs[:, c:d], 0.0, A.is_equal, keys("x", c, d), keys("m", c, d), n="M%d" % c)
-        cp(T.mk[:].indirect(FIRST), T.zero[:], "l5 zero", keys("m", 0, M), "R%d" % a)
         scan(T.ff[:, a + 1:b + 1], T.mk[:, a:b], T.xs[:, a:b], T.ff[:, a:a + 1] if a else 0.0,
              "ff " + keys("m", a, b) + " " + keys("x", a, b), "ff", "F%d" % a)
     fw = T.ff[:]
@@ -310,8 +334,7 @@ def rank_program(g, core, T, topo):
         total["loc"] += len(common(r))
     for n in range(N):
         move["vs"[n % 2]](blk(T.a, n), fw.indirect(T.offf[:, 12 * n:12 * n + 12]), "ff ffp offf", "oa%d" % n)
-    for n, p in enumerate(peers):
-        send("A%d" % n, p, blk(T.a, 4 + peers_of(p).index(r)), blk(T.a, n), "ra", "oa%d" % n)
+    send("A", AC, "ra", lambda n: (blk(T.a, 4 + there(n)), blk(T.a, n), "oa%d" % n))
 
     lin(T.slf[:, 32:64], QI, 4.0, 0.0, "qtr", "qi4")
     tt(T.slf[:, 64:96], T.slf[:, 32:64], SI, A.add, "qtr qi4", "cof")
@@ -325,8 +348,8 @@ def rank_program(g, core, T, topo):
     for h in range(2):
         c = slice(512 * h, 512 * (h + 1))
         odd = slice(512 * h + 1, 512 * (h + 1), 2)
-        move["sv"[h]](T.iv[:, 512 * h:512 * (h + 1):2], T.cw[:].indirect(T.coff[:, 16 * h:16 * (h + 1)]), "cw coff", "cz%d" % h)
-        move["sv"[h]](T.iv[:, odd], T.a[:, 576:1344].indirect(T.slot[:, 16 * h:16 * (h + 1)]), "lar oa3 slot", "v%d" % h)
+        move[CZ[h]](T.iv[:, 512 * h:512 * (h + 1):2], T.cw[:].indirect(T.coff[:, 16 * h:16 * (h + 1)]), "cw coff", "cz%d" % h)
+        move[VV[h]](T.iv[:, odd], T.a[:, 576:1344].indirect(T.slot[:, 16 * h:16 * (h + 1)]), "lar oa3 slot", "v%d" % h)
         ts(T.zv[:, odd], T.iv[:, odd], 0.0, A.is_equal, "zv v%d" % h, "zv%d" % h)
         scan(T.ov[:, c], T.zv[:, c], T.iv[:, c], 0.0, "zv zv%d v%d cz%d" % (h, h, h), "ov%d" % h)
         move["vs"[h]](T.yo[:, 256 * h:256 * (h + 1)], T.ov[:, odd], "ov%d" % h, "yo%d" % h)
@@ -334,7 +357,7 @@ def rank_program(g, core, T, topo):
 
     todo = {e: [n for n in ORDER[e].split() if n in steps] for e in ORDER}
     assert sorted(n for e in todo for n in todo[e]) == sorted(steps) and all(steps[n][0] == e for e in todo for n in todo[e])
-    done, seen = {s: (s, total[s]) for s in ("qa", "la", "ra")}, {}
+    done, seen = {s: (s, total[s]) for s in ("qa", "ia", "la", "ra")}, {}
     group = {s: [n for n in steps if steps[n][2] == s] for s in total}
 
     def wait(e, s, v):

from concourse.bass import DstId, RemoteDMATransfer
from concourse.mybir import AluOpType as A, ActivationFunctionType as F

M, Q, CAP, W = 4096, 512, 192, 65536
PAD = M + 256
BIG = float(2 ** 20)
RND = 1.5 * 2 ** 23
BF, F32, I32, U16 = "bfloat16", "float32", "int32", "uint16"
COLS = {
    BF: dict(one=128, kn=128, bb=128, b12=128, lin=128, eye=128, z=144, z0=144, za1=144, za2=144, pcs=96, oh=136, rst=136,
             sc=136, rows=512, u=1344, tp=512, tw=M, tsw=PAD, nb0=128, nb=128, pen=640, pa=256, pd=128, fs=128, xw=M, xs=M,
             mk=PAD, ff=PAD, ca=768, cb=768, a=1344, lo=128, ll=384, il=512, zl=512, cw=512, iv=1024, zv=1024,
             ov=1024, yo=512, zero=128, ul=96),
    F32: dict(pf=8, c0=32, cd=128, cr=160, ct=160, qf=96, qtr=96, prod=136, t1=72, slf=96, sf=136, sx=128, dj=8, em=32, lf=64,
              bbf=128, ub=128, kwa=264, kwb=264, pen5=128, ta1=128, ta2=640, qw=768, g2=768),
    I32: dict(qp=128, qn=32, qm=96, tb=256, pmi=256, srow=136),
    U16: dict(slot=32, coff=32, pmu=256, l5=64, offa=48, offb=48, offf=48),
}
PS = ("pk", "pk2", "pq1", "pq2", "pb", "pp", "pi", "pfi")
SCRATCH = {n: ("sbuf", [128, c], d) for d in COLS for n, c in COLS[d].items()}
SCRATCH.update({n: ("psum", [128, 512], F32) for n in PS})
SEMAPHORES = ["ev", "es", "et", "eg", "qa", "ia", "la", "ra", "loc"] + ["d%d" % k for k in range(20)]
XA = 512
TCH = ((0, 1024, "s"), (1024, 2048, "s"), (2048, 2816, "s"), (3072, M, "v"), (2816, 3072, "v"))
XCH = ((0, 512, "s"), (512, 1024, "s"), (1024, 2048, "s"), (2048, 3072, "s"), (3072, 3584, "v"), (3584, M, "v"))
MCH = ((0, 1024), (1024, 2048), (2048, 3072), (3072, 3584), (3584, M))
FCH = ((0, 3072), (3072, M))
CZ = "sv"
VV = "sv"
QC = ((0,), (1,), (2,))
IC = ((0, 1, 2),)
AC = ((0,), (1,), (2,))
ORDER = dict(
    y="Ltb Lst0 Lst1 Lst2 Lst3 Lpm Lsrow Dtw0 Dtw1 Drow0 Drow1 Drow2 Lxa Lxb Y0",
    s="Lqt0 Lqt1 Lqn Lqm Lqi0 Lqi1 tw0 tw1 tw2 tw3 tph bbf rst sw rst0 b0 b0x sx lf0 lf1 lf2 lf3 lf4 b16 T0 T2048 T1024 "
      "ba pc ub ul pa pd nb pen1 pen2 pen3 pen4 X0 X512 qw0 qw1 X2048 X1024 za2 g20 g21 lo oa1 qi4 oa3 il2 il3 cz0 v0 yo1 Y1",
    v="st rows sw2 srow tw4 tpf low hi si pcs qf tpl qtr sf oh0 oh1 oh2 oh3 em sc ed pmu prod lf6 t1 lf5 slf l5 slot scat "
      "cr0 T3072 ct T2816 X3072 kwb fs X3584 pen5 pen0 M3584 ta1 M3072 offa M0 ca kwa M2048 ta2 offb M1024 R0 cb0 F0 cb1 F3072 offf "
      "oa0 oa2 cof coff zl2 il1 zl3 cw cz1 v1 zv1 zv0 ov1 ov0 yo0",
    t="bc0 slotm bc K0 pi P191 P0 P124 K3072 pfi q1 q2 K1024 K2048 pb pp1 pp2",
    g="one z c0 ohl bb0 bb dj lin kn zs cd0 cd1 cd2 cd3 pad cd4 cr1 cr2 cr3 z0 Q0 Q1 Q2 I0 eye b12 zero za1 zl il0 zv ffp ff "
      "L A0 A1 A2",
)


def rank_program(g, core, T, topo):
    r = T.rank_of(core)
    if r is None:
        return
    cores = list(T.cores)
    N = len(cores)
    qs = {"v": g.vector, "s": g.scalar, "t": g.tensor, "g": g, "y": g.sync}
    esem = {"v": "ev", "s": "es", "t": "et", "g": "eg"}
    steps, wr, rd, bank, total = {}, {}, {}, {}, {"loc": 0}

    def step(name, e, fn, R, Wr, sem, more=False):
        R, Wr = R.split(), Wr.split()
        dep = {t for k in R + Wr for t in wr.get(k, [])} | {t for k in Wr for t in rd.get(k, [])}
        if more:
            dep = {t for t in dep if t in total or steps[t][0] != e}
        for k in R + Wr:
            b = k.split(":")[0]
            if b in PS:
                dep |= {t for t in bank.setdefault(b, []) if steps[t][0] != e}
        for b in {k.split(":")[0] for k in R + Wr} & set(PS):
            bank[b].append(name)
        for k in R:
            rd.setdefault(k, []).append(name)
        for k in Wr:
            wr[k], rd[k] = [name], []
        assert name not in steps, name
        steps[name] = (e, fn, sem, dep)

    def op(e, fn, R, Wr, n=None, more=False):
        step(n or Wr.split()[0], e, fn, R, Wr, esem[e], more)

    def dmas(items):
        s = "d%d" % len(total)
        total[s] = 16 * len(items)
        was = {k: (wr.get(k, []), rd.get(k, [])) for it in items for k in it[5].split()}
        for n, e, o, i, R, Wr in items:
            for k in Wr.split():
                wr[k], rd[k] = was[k]
            step(n, e, lambda e=e, o=o, i=i: qs[e].dma_start(o, i), R, Wr, s)

    V, SC, PE = g.vector, g.scalar, g.tensor

    def ts(o, i, a, o0, R, Wr, b=None, o1=None, n=None):
        op("v", lambda: V.tensor_scalar(o, i, a, None, o0) if b is None else V.tensor_scalar(o, i, a, b, o0, o1), R, Wr, n)

    def tt(o, a, b, o0, R, Wr, n=None):
        op("v", lambda: V.tensor_tensor(o, a, b, o0), R, Wr, n)

    def cp(o, i, R, Wr, n=None):
        op("v", lambda: V.tensor_copy(o, i), R, Wr, n)

    def ms(o, c, Wr):
        op("v", lambda: V.memset(o, c), "", Wr)

    def turn(o, i, R, Wr):
        op("v", lambda: V.transpose(o, i), R, Wr)

    def scan(o, a, b, ini, R, Wr, n=None):
        op("v", lambda: V.tensor_tensor_scan(o, a, b, ini, A.mult, A.add), R, Wr, n)

    def act(o, i, R, Wr, n=None):
        op("s", lambda: SC.activation(o, i, F.Copy), R, Wr, n)

    def lin(o, i, sc, bi, R, Wr, f=F.Identity, n=None):
        op("s", lambda: SC.activation(o, i, f, scale=sc, bias=bi), R, Wr, n)

    def iota(o, pat, base, Wr, cm=0):
        op("g", lambda: g.iota(o, pat, base, cm, allow_small_or_imprecise_dtypes=True), "", Wr)

    def sel(o, i, pat, cmp, base, cm, R, Wr, fill=0.0, n=None):
        op("g", lambda: g.affine_select(o, i, pat, cmp, fill, base, cm), R, Wr, n)

    def mm(n, calls, R, Wr):
        op("t", lambda: [PE.matmul(*c) for c in calls][-1], R, Wr, n, not calls[0][3])

    def spread(out, z, src, lo, hi, first, last):
        return [(out, z[:, 15 - k:143 - k], src[:, lo + k:hi:16], first and k == 0, last and k == 15) for k in range(16)]
    move = {"s": act, "v": cp}

    def peers_of(a):
        def far(p):
            x, y = topo.chip(cores[a]), topo.chip(cores[p])
            return 3 if x == y else 2 if topo.mates(x, y) else 1 if topo.same_plane(x, y) else 0
        return sorted([p for p in range(N) if p != a], key=far)
    peers = peers_of(r)

    def common(a):
        return [e for e in topo.engines(cores[a], cores[(a + 1) % N])
                if all(e in topo.engines(cores[a], cores[b]) for b in range(N) if b != a)]

    def shares(a, call):
        es, out = common(a), []
        for k in range(len(call)):
            n = len(es) if k == len(call) - 1 else len(es) // 2
            out.append(es[:n])
            es = es[n:]
        return out

    def send(name, calls, sem, part):
        for call in calls:
            trs = []
            for n, es in zip(call, shares(r, call)):
                rid, pid, se = topo.addr(cores[peers[n]])
                trs.append(RemoteDMATransfer(dst_ids=[DstId(rid=rid, pnc=pid)], dma_engine_mask=sum(1 << e for e in es),
                                             remote_sem=T.sem[sem], src=part(n)[1], dst=part(n)[0]))
            step("%s%d" % (name, call[0]), "g", lambda trs=trs: g.remote_dma_fused(trs, local_sem=T.sem.loc),
                 " ".join(part(n)[2] for n in call), "", None)
            total["loc"] += len(common(r))
        total[sem] = sum(len(es) for p in peers for call in calls for n, es in zip(call, shares(p, call)) if peers_of(p)[n] == r)

    def there(n):
        return peers_of(peers[n]).index(r)

    def blk(t, n):
        return t[:, CAP * n:CAP * (n + 1)]

    def keys(n, a, b):
        return " ".join("%s.%d" % (n, c) for c in range(a // 256, (b + 255) // 256))
    total.update(qa=0, ia=0, ra=0)
    total["la"] = sum(len(common(p)) for p in peers if p < N - 1)
    wr.update(lqr=["qa"], lqi=["ia"], llr=["la"], lar=["ra"])

    ms(T.qp[:, 64:96], 0, "st")
    ms(T.srow[:], 0, "srow")
    dmas([("Ltb", "y", T.tb[:], T.times[:], "", "tb")])
    dmas([("Lqt%d" % h, "s", T.qp[:, 16 * h:16 * h + 16], T.qt[h::2, :], "", "qt") for h in range(2)])
    dmas([("Lsrow", "y", T.srow[0::16, 0:129], T.starts[:], "", "srow")])
    dmas([("Lqi%d" % h, "s", T.qp[:, 32 + 16 * h:48 + 16 * h], T.qi[h::2, :], "", "qi") for h in range(2)]
         + [("Lst%d" % (2 * e + h), "y", T.qp[e::4, 64 + 16 * h:80 + 16 * h], T.starts[h::2, e:128 + e], "", "st")
            for e in range(2) for h in range(2)])
    dmas([("Lqn", "s", T.qn[:], T.qt[:], "", "qn"), ("Lqm", "s", T.qm[:, 0:32], T.qi[:], "", "qn")])
    dmas([("Lpm", "y", T.pmi[:], T.pm[:], "", "pmi")])
    dmas([("Lxa", "y", T.xw[:, 0:XA], T.x[:, 0:XA], "", "xwa")])
    dmas([("Lxb", "y", T.xw[:, XA:M], T.x[:, XA:M], "", "xwb")])
    ms(T.rows[:], 0.0, "rows")
    for c in range(4):
        n = 512 if c < 3 else 256
        act(T.tw[:, 512 * c:512 * c + n], T.rows[:, 0:n], "rows", "tw%d" % c)
    ms(T.tw[:, 1792:M], 0.0, "tw4")
    TW = "tw0 tw1 tw2 tw3 tw4"
    lin(T.rst[:], T.rows[:, 0:136], 0.0, 1.0, "rows", "rst")
    act(T.u[:, 576:960], T.rows[:, 0:384], "rows", "sw")
    ms(T.u[:, 960:1344], 0.0, "sw2")
    iota(T.tsw[:, M:PAD], [[0, PAD - M]], W, "pad")
    iota(T.one[:], [[0, 128]], 1, "one")
    sel(T.bb[:], T.one[:], [[-16, 8], [0, 16]], A.is_ge, 0, 1, "one", "bb", n="bb0")
    sel(T.bb[:], T.bb[:], [[16, 8], [0, 16]], A.is_ge, 15, -1, "bb", "bb")
    sel(T.lin[:], T.bb[:], [[1, 128]], A.is_gt, 0, -1, "bb", "lin")
    iota(T.oh[:, 0:132:33], [[12, 4]], 0, "ohl")
    lin(T.rst[:, 0:132:33], T.oh[:, 0:132:33], 0.0, 0.0, "ohl", "rst", n="rst0")
    iota(T.z[:], [[0, 144]], 0, "z")
    sel(T.z[:, 15:143:16], T.bb[:, 0::16], [[0, 8]], A.is_ge, 0, 0, "bb", "z", n="zs")
    iota(T.kn[0:1, :], [[0, 8], [-1, 16]], 7, "kn")
    iota(T.dj[:], [[16, 8]], M + 1, "dj", 1)
    sel(T.b12[:], T.bb[:], [[-16, 8], [0, 16]], A.not_equal, 0, 1, "bb", "b12")
    sel(T.z0[:], T.z[:], [[1, 144]], A.is_equal, -15, -1, "z", "z0")
    sel(T.eye[:], T.bb[:], [[1, 128]], A.is_equal, 0, -1, "bb", "eye")
    sel(T.za1[:], T.z[:], [[1, 144]], A.is_ge, -12, -1, "z", "za1")
    iota(T.zero[:], [[0, 128]], 0, "zero")
    iota(T.ff[:, M + 1:PAD], [[0, PAD - M - 1]], 0, "ffp")
    iota(T.ff[:, 0:1], [[0, 1]], 0, "ff")
    iota(T.il[:, 0::4], [[0, 128]], 0, "il0")
    iota(T.zl[:], [[0, 512]], 0, "zl zl2 zl3")
    iota(T.zv[:, 0::2], [[0, 512]], 0, "zv")
    K, KN = [[0, 2], [1, 16]], [[0, 2], [-1, 16]]
    iota(T.c0[:], [[0, 32]], 0, "c0")
    sel(T.cd[:, 0:32], T.c0[:], KN, A.is_ge, 5, 0, "c0", "cd0", 2.0)
    sel(T.cd[:, 32:64], T.c0[:], KN, A.is_ge, 5, 0, "c0", "cd1", 0.5)
    sel(T.cd[:, 64:96], T.c0[:], K, A.is_ge, -6, 0, "c0", "cd2", 16.0)
    sel(T.cd[:, 96:128], T.c0[:], K, A.not_equal, -5, 0, "c0", "cd3", -2.0 ** 27)
    sel(T.cd[:, 64:96], T.cd[:, 64:96], K, A.not_equal, -4, 0, "cd2", "cd2", -8192.0, "cd4")
    sel(T.cr[:, 64:96], T.c0[:], KN, A.is_ge, 4, 0, "c0", "cr1", 2.0 ** 35 + 2.0 ** 17)
    sel(T.cr[:, 96:128], T.c0[:], K, A.is_ge, -4, 0, "c0", "cr2", -BIG)
    iota(T.cr[:, 128:160], [[0, 2], [-15, 16]], -17, "cr3")
    scan(T.cr[:, 0:64], T.cd[:, 0:64], T.cd[:, 64:128], 0.0, "cd0 cd1 cd2 cd3", "cr0")
    turn(T.ct[:], T.cr[:], "cr0 cr1 cr2 cr3", "ct")
    WA2, SU, BU, SA, N17 = [T.ct[:, 32 * k:32 * k + 1] for k in range(5)]
    BA = T.pf[:, 0:1]
    lin(BA, N17, SA, 0.0, "ct", "ba")
    lin(T.za2[:], T.z[:], WA2, 0.0, "z ct", "za2")

    ts(T.qp[:, 96:128], T.qp[:, 0:32], 16, A.arith_shift_right, "qt", "si")
    ts(T.qm[:, 32:64], T.qn[:], 0xFF00, A.bitwise_and, "qn", "hi")
    ts(T.qm[:, 64:96], T.qn[:], 0xFF, A.bitwise_and, "qn", "low")
    cp(T.pcs[:], T.qm[:], "qn hi low", "pcs")
    dmas([("Drow%d" % k, "y", T.rows[k::16, :], T.pcs[:, 32 * k:32 * k + 32], "pcs", "rows") for k in range(3)])
    cp(T.qf[:], T.qp[:, 32:128], "qi st si", "qf")
    turn(T.qtr[:], T.qf[:], "qf", "qtr")
    QI, ST, EN, SI = T.qtr[:, 0:32], T.qtr[:, 32:64:4], T.qtr[:, 33:64:4], T.qtr[:, 64:96]
    for b, s in enumerate([r] + peers):
        ts(T.oh[:, 33 * b + 1:33 * b + 33], SI, float(s), A.is_equal, "qtr", "oh%d" % b)
    ohk = "ohl oh0 oh1 oh2 oh3"
    scan(T.sc[:, 0:132], T.rst[:, 0:132], T.oh[:, 0:132], 0.0, "rst " + ohk, "sc")
    mm("slotm", [(T.pi[:, 0:131], T.lin[:], T.oh[:, 1:132], True, False), (T.pi[:, 0:131], T.bb[:], T.sc[:, 0:131], False, True)],
       "lin bb sc " + ohk, "pi")
    tt(T.prod[:, 0:131], T.pi[:, 0:131], T.oh[:, 1:132], A.mult, "pi " + ohk, "prod")
    tt(T.t1[:, 0:65], T.prod[:, 0:65], T.prod[:, 66:131], A.add, "prod", "t1")
    tt(T.slf[:, 0:32], T.t1[:, 0:32], T.t1[:, 33:65], A.add, "t1", "slf")
    cp(T.slot[:], T.slf[:, 0:32], "slf", "slot")
    cp(T.u[:, 576:1344].indirect(T.slot[:]), T.rows[:], "slot rows", "sw sw2", "scat")
    send("Q", QC, "qa", lambda n: (blk(T.u, there(n)), blk(T.u, 4 + n), "sw"))
    mm("pi", spread(T.pi[:, 0:48], T.z0, T.u, 576, 1344, True, True), "z0 sw sw2", "pi")
    lin(T.ul[:, 40:88], T.pi[:, 0:48], 1.0 / 128, 0.0, "pi", "ul")
    send("I", IC, "ia", lambda n: (T.ul[:, 4 + 12 * there(n):16 + 12 * there(n)], T.ul[:, 52 + 12 * n:64 + 12 * n], "ul"))

    ts(T.pfi[:, 0:256], T.tb[:], float(r * W), A.subtract, "tb", "pfi", n="tpf")
    act(T.tp[:, 0:256], T.pfi[:, 0:256], "pfi", "tph")
    tt(T.tp[:, 256:512], T.pfi[:, 0:256], T.tp[:, 0:256], A.subtract, "pfi tph", "tpl")
    dmas([("Dtw0", "y", T.tw[0::16, :], T.tp[:, 0:256], "tph", TW), ("Dtw1", "y", T.tw[1::16, :], T.tp[:, 256:512], "tpl", TW)])
    cp(T.pmu[:], T.pmi[:], "pmi", "pmu")
    for a, b, e in TCH:
        move[e](T.tsw[:, a:b], T.tw[:].indirect(T.pmu[:, a // 16:b // 16]), TW + " pmu", keys("t", a, b), "T%d" % a)
    for a in range(0, M, 1024):
        b = a + 1024 + (128 if a == 3072 else 0)
        mm("K%d" % a, spread(T.pk[:, a // 16:b // 16], T.z, T.tsw, a, b, True, True), "z pad " + keys("t", a, b), "pk:%d" % a)
    for a, b in ((0, 124), (124, 191), (191, 258)):
        mm("P%d" % a, [(T.pk2[:, a:b], T.z[:, 15 - k:143 - k], T.tsw[:, 16 * (a + k + 1):16 * (b + k) + 1:16], k == 0, k == 3)
                       for k in range(4)], "z pad " + keys("t", 16 * (a + 1), 16 * (b + 3) + 1), "pk2:%d" % a)
    cp(T.kwa[:], T.pk[:, 0:264], "pk:0 pk:1024 pk:2048 pk:3072", "kwa")
    cp(T.kwb[:, 0:258], T.pk2[:, 0:258], "pk2:0 pk2:124 pk2:191", "kwb")
    ts(T.sf[:], T.srow[:], 7.0 / 16, A.subtract, "srow", "sf")
    act(T.bbf[:], T.bb[:], "bb", "bbf")
    mm("bc0", [(T.pq2[:, 0:128], T.bbf[:], T.sf[:, 0:128], True, True)], "bbf sf", "pq2")
    lin(T.sx[:], T.pq2[:, 0:128], (1 - 2.0 ** -13) / 16, RND, "pq2", "sx")
    lin(T.nb0[:], T.sx[:], -1.0, RND, "sx", "b16")
    mm("bc", [c for h in range(2) for c in ((T.pp[:, 128 * h:128 * h + 128], T.bbf[:], T.sf[:, h:128 + h], True, False),
                                            (T.pp[:, 128 * h:128 * h + 128], T.bb[:], T.nb0[:], False, False),
                                            (T.pp[:, 128 * h:128 * h + 128], T.kn[0:1, :], T.one[0:1, :], False, True))],
       "bb bbf kn one sf b16", "pp")
    lin(T.em[:, 0:8], ST, 1.0 / 16, -7.5 / 16, "qtr", "b0")
    lin(T.em[:, 8:16], T.em[:, 0:8], 1.0, RND, "b0", "b0x")
    for c in range(5):
        lin(T.lf[:, 8 * c:8 * c + 8], T.em[:, 8:16], 1.0, c - RND, "b0x", "lf%d" % c)
    tt(T.em[:, 16:24], EN, ST, A.is_le, "qtr", "em")
    tt(T.em[:, 24:32], T.em[:, 16:24], T.dj[:], A.mult, "em dj", "ed")
    tt(T.lf[:, 40:48], T.em[:, 24:32], ST, A.max, "ed qtr", "lf5")
    tt(T.lf[:, 48:56], T.em[:, 24:32], EN, A.max, "ed qtr", "lf6")
    cp(T.l5[:, 0:56], T.lf[:, 0:56], "lf0 lf1 lf2 lf3 lf4 lf5 lf6", "l5")
    FIRST, END = T.l5[:, 40:48], T.l5[:, 48:56]
    D = T.pp[:, 128:256]
    lin(T.pb[:, 0:128], D, -BIG, BIG, "pp", "pb", F.Relu, "pa")
    lin(T.pa[:, 128:256], T.pp[:, 0:128], BIG, 0.0, "pp", "pc", F.Relu)
    tt(T.pen[:, 0:128], T.pb[:, 0:128], T.pa[:, 128:256], A.subtract, "pb pc", "pen0")
    for c in range(1, 5):
        lin(T.pen[:, 128 * c:128 * (c + 1)], D, -BIG, BIG * (16 * c + 1), "pp", "pen%d" % c, F.Relu)
    tt(T.ta2[:], T.kwa[:].indirect(T.l5[:, 0:40]), T.pen[:], A.add, "kwa l5 pen0 pen1 pen2 pen3 pen4", "ta2")
    cp(T.fs[:], T.tsw[:].indirect(FIRST), keys("t", 0, M) + " pad l5", "fs")
    lin(T.pd[:], D, SA, BA, "pp ct ba", "pd", F.Relu)
    lin(T.ub[:], T.nb0[:], SU, BU, "b16 ct", "ub")
    lin(T.nb[:], T.ub[:], -1.0, 0.0, "ub", "nb")
    mm("pfi", [(T.pfi[:, 0:128], T.eye[:], T.pd[:], True, False), (T.pfi[:, 0:128], T.eye[:], T.nb[:], False, False),
               (T.pfi[:, 0:128], T.z[:, 11:139], T.fs[:], False, True)], "eye pd nb z fs", "pfi")
    tt(T.pen5[:], T.pfi[:, 0:128], T.ub[:], A.add, "pfi ub", "pen5")
    tt(T.ta1[:], T.kwb[:, 0:258].indirect(T.l5[:, 0:8]), T.pen5[:], A.add, "kwb l5 pen5", "ta1")
    mm("q1", [(T.pq1[:, 0:384], T.b12[:], T.u[:, 0:384], True, True)], "b12 sw lqr", "pq1")
    mm("q2", [(T.pq2[:, 0:384], T.b12[:], T.u[:, 384:768], True, True)], "b12 sw lqr", "pq2")
    act(T.qw[:, 0:384], T.pq1[:, 0:384], "pq1", "qw0")
    act(T.qw[:, 384:768], T.pq2[:, 0:384], "pq2", "qw1")
    ts(T.offa[:], T.ul[:, 4:52], 128.0, A.mult, "ul lqi", "offa")
    tt(T.ca[:], T.ta1[:].indirect(T.offa[:]), T.qw[:], A.is_le, "ta1 offa qw0 qw1", "ca")
    mm("pb", [(T.pb[:, 0:48], T.eye[:], T.ul[:, 4:52], True, False)] + spread(T.pb[:, 0:48], T.za1, T.ca, 0, 768, False, True),
       "eye ul lqi za1 ca", "pb")
    mm("pp1", spread(T.pp[:, 0:48], T.za2, T.ca, 0, 768, True, False), "za2 ca", "pp")
    ts(T.offb[:], T.pb[:, 0:48], 128.0, A.mult, "pb", "offb")
    for h in range(2):
        c = slice(384 * h, 384 * h + 384)
        act(T.g2[:, c], T.ta2[:].indirect(T.offb[:, 24 * h:24 * h + 24]), "ta2 offb", "g2%d" % h)
        tt(T.cb[:, c], T.g2[:, c], (T.pq1, T.pq2)[h][:, 0:384], A.is_le, "g2%d pq%d" % (h, h + 1), "cb%d" % h)
    mm("pp2", spread(T.pp[:, 0:48], T.z, T.cb, 0, 768, False, True), "z cb0 cb1", "pp")
    ts(T.offf[:], T.pp[:, 0:48], 8192.0, A.add, "pp", "offf", float(M + 1), A.min)
    for a, b, e in XCH:
        move[e](T.xs[:, a:b], T.xw[:].indirect(T.pmu[:, a // 16:b // 16]), "xwa xwb pmu", keys("x", a, b), "X%d" % a)
    for c, d in MCH:
        ts(T.mk[:, c:d], T.xs[:, c:d], 0.0, A.is_equal, keys("x", c, d), keys("m", c, d), n="M%d" % c)
    cp(T.mk[:].indirect(FIRST), T.zero[:], "l5 zero", keys("m", 0, M), "R0")
    for a, b in FCH:
        scan(T.ff[:, a + 1:b + 1], T.mk[:, a:b], T.xs[:, a:b], T.ff[:, a:a + 1] if a else 0.0,
             "ff " + keys("m", a, b) + " " + keys("x", a, b), "ff", "F%d" % a)
    fw = T.ff[:]

    def last(s):
        return T.lo[:] if s == r else T.ll[:, 128 * s:128 * s + 128]
    if r < N - 1:
        act(T.lo[:], fw.indirect(END), "ff ffp l5", "lo")
        to = [DstId(rid=topo.addr(cores[p])[0], pnc=topo.addr(cores[p])[1]) for p in peers]
        tr = RemoteDMATransfer(dst_ids=to, dma_engine_mask=sum(1 << e for e in common(r)), remote_sem=T.sem.la,
                               src=T.lo[:], dsts=[T.ll[:, 128 * r:128 * r + 128]] * len(peers))
        step("L", "g", lambda: g.remote_dma_fused([tr], local_sem=T.sem.loc), "lo", "", None)
        total["loc"] += len(common(r))
    for n in range(N):
        move["vs"[n % 2]](blk(T.a, n), fw.indirect(T.offf[:, 12 * n:12 * n + 12]), "ff ffp offf", "oa%d" % n)
    send("A", AC, "ra", lambda n: (blk(T.a, 4 + there(n)), blk(T.a, n), "oa%d" % n))

    lin(T.slf[:, 32:64], QI, 4.0, 0.0, "qtr", "qi4")
    tt(T.slf[:, 64:96], T.slf[:, 32:64], SI, A.add, "qtr qi4", "cof")
    cp(T.coff[:], T.slf[:, 64:96], "cof", "coff")
    for s in range(N - 1):
        k = "lo" if s == r else "llr"
        if s:
            ts(T.zl[:, s + 1::4], last(s), 0.0, A.is_equal, k, "zl%d" % (s + 1))
        (cp if s == 0 else act)(T.il[:, s + 1::4], last(s), k, "il%d" % (s + 1))
    scan(T.cw[:], T.zl[:], T.il[:], 0.0, "il0 il1 il2 il3 zl zl2 zl3", "cw")
    for h in range(2):
        c = slice(512 * h, 512 * (h + 1))
        odd = slice(512 * h + 1, 512 * (h + 1), 2)
        move[CZ[h]](T.iv[:, 512 * h:512 * (h + 1):2], T.cw[:].indirect(T.coff[:, 16 * h:16 * (h + 1)]), "cw coff", "cz%d" % h)
        move[VV[h]](T.iv[:, odd], T.a[:, 576:1344].indirect(T.slot[:, 16 * h:16 * (h + 1)]), "lar oa3 slot", "v%d" % h)
        ts(T.zv[:, odd], T.iv[:, odd], 0.0, A.is_equal, "zv v%d" % h, "zv%d" % h)
        scan(T.ov[:, c], T.zv[:, c], T.iv[:, c], 0.0, "zv zv%d v%d cz%d" % (h, h, h), "ov%d" % h)
        move["vs"[h]](T.yo[:, 256 * h:256 * (h + 1)], T.ov[:, odd], "ov%d" % h, "yo%d" % h)
        dmas([("Y%d" % h, "ys"[h], T.y[:, 256 * h:256 * (h + 1)], T.yo[:, 256 * h:256 * (h + 1)], "yo%d" % h, "")])

    todo = {e: [n for n in ORDER[e].split() if n in steps] for e in ORDER}
    assert sorted(n for e in todo for n in todo[e]) == sorted(steps) and all(steps[n][0] == e for e in todo for n in todo[e])
    done, seen = {s: (s, total[s]) for s in ("qa", "ia", "la", "ra")}, {}
    group = {s: [n for n in steps if steps[n][2] == s] for s in total}

    def wait(e, s, v):
        if seen.get((e, s), 0) < v:
            qs[e].wait_ge(T.sem[s], v)
            seen[(e, s)] = v

    def ready(n):
        return all(m in done for t in steps[n][3] for m in (group.get(steps[t][2], [t]) if t in steps else [t]))
    while any(todo.values()):
        e = [e for e in todo if todo[e] and ready(todo[e][0])][0]
        n = todo[e].pop(0)
        fn, s, dep = steps[n][1:]
        need = {}
        for t in dep:
            need[done[t][0]] = max(need.get(done[t][0], 0), done[t][1])
        for t in sorted(need):
            wait(e, t, need[t])
        call = fn()
        if s in esem.values():
            total[s] = total.get(s, 0) + 1
        if s:
            call.then_inc(T.sem[s], 1 if s in esem.values() else 16)
        done[n] = (s, total.get(s))
    for s in total:
        wait("g", s, total[s])
